import numpy as np
import ml_dtypes


def mxq(x, axis, fmt="e4m3"):
    dtype, down = {"e4m3": (ml_dtypes.float8_e4m3fn, 7), "e5m2": (ml_dtypes.float8_e5m2, 14)}[fmt]
    v = np.moveaxis(np.asarray(x, np.float32).astype(ml_dtypes.bfloat16).astype(np.float64), axis, -1)
    blocks = v.reshape(v.shape[:-1] + (-1, 32))
    amax = np.abs(blocks).max(-1, keepdims=True)
    byte = np.maximum(np.where(amax > 0, np.frexp(amax)[1] - 1 + 127, 0) - down, 1)
    scale = np.exp2(byte - 127.0)
    codes = (blocks / scale).astype(np.float32).astype(dtype).astype(np.float64)
    return np.moveaxis((codes * scale).reshape(v.shape), -1, axis)


WIDE = False


def mx_kscale(k):
    if not WIDE:
        return np.ones(k)
    levels = np.array([10, -10, 5, -5, 0])
    if k % 512:
        return np.exp2(np.random.permutation(np.resize(levels, k // 32))).repeat(32)
    a = np.empty((k // 512, 16))
    for p in range(k // 512):
        a[p, :8] = np.random.permutation(np.resize(levels, 8))
        for g in range(8):
            far = levels[np.abs(levels - a[p, g]) >= 10]
            a[p, g + 8] = far[np.random.randint(len(far))]
    return np.exp2(a.ravel()).repeat(32)


BF16 = ml_dtypes.bfloat16


def bf(x):
    return np.asarray(x, np.float32).astype(BF16)


def f64(x):
    return np.asarray(x).astype(np.float64)

E4M3FN = np.array([(-1.0 if i & 128 else 1.0) * ((1.0 + (i & 7) / 8.0) * 2.0 ** (((i >> 3) & 15) - 7) if i & 120 else (i & 7) * 2.0 ** -9) for i in range(256)])


def e4m3fn_bytes(y):
    return np.clip(np.asarray(y, np.float64), -448.0, 448.0).astype(np.float32).astype(ml_dtypes.float8_e4m3fn).view(np.uint8)


def e4m3fn_values(b):
    return E4M3FN[b]

def planes(Y):
    n, m = Y.shape
    b = f64(bf(Y)).reshape(n // 32, 32, m)
    amax = np.abs(b).max(1)
    byte = np.clip(np.where(amax > 0, np.frexp(amax)[1] - 1 + 127 - 7, 1), 1, 254)
    codes = (b * np.exp2(127.0 - byte)[:, None, :]).reshape(n, m).astype(np.float32).astype(ml_dtypes.float8_e4m3fn).view(np.uint8)
    words = codes.reshape(n // 512, 128, 4, m).transpose(0, 1, 3, 2)
    return np.ascontiguousarray(words), np.ascontiguousarray(byte.astype(np.uint8).reshape(n // 512, 16, m))


S, D, H, T, B = 4096, 512, 16, 64, 128


def setup_inputs():
    s = mx_kscale(D)
    size = np.exp(0.8 * np.random.randn(S, 1))
    keys = (0.5 * np.random.randn(1, D) + size * np.random.randn(S, D)) * s
    keys_mean = bf(keys.mean(axis=0, keepdims=True))
    centred = keys - f64(keys_mean)
    keys_scale = (np.abs(centred).reshape(S, D // B, B).max(axis=2) / 448.0).astype(np.float32)
    keys_bytes = e4m3fn_bytes(centred / np.repeat(f64(keys_scale), B, axis=1))
    queries = bf(np.random.randn(H, T, D) / s)
    temp = bf(np.exp(0.3 * np.random.randn(H, T, 1)) / np.sqrt(D))
    cap = bf(4.0 * np.exp(0.4 * np.random.randn(H, 1, 1)))
    return {"keys_bytes": keys_bytes, "keys_scale": keys_scale, "keys_mean": keys_mean,
            "queries": queries, "temp": temp, "cap": cap}

def reference(keys_bytes, keys_scale, keys_mean, queries, temp, cap):
    keys = e4m3fn_values(keys_bytes) * np.repeat(f64(keys_scale), B, axis=1) + f64(keys_mean)
    kq = mxq(keys, 1, "e4m3")
    qq = mxq(f64(queries).reshape(H * T, D), 1, "e4m3")
    raw = (qq @ kq.T).reshape(H, T, S)
    c = f64(cap)
    y = c * np.tanh(raw * f64(temp) / c)
    Y = y.reshape(H * T, S).T
    words, scales = planes(Y)
    return y, words, scales

@@ -1,0 +1,354 @@
+from contextlib import ExitStack
+
+import concourse.mybir as mybir
+from concourse.masks import make_identity
+
+S, D, H, T, B = 4096, 512, 16, 64, 128
+FLOPS = 2 * H * T * S * D
+
+F32 = mybir.dt.float32
+BF16 = mybir.dt.bfloat16
+I32 = mybir.dt.int32
+U32 = mybir.dt.uint32
+U8 = mybir.dt.uint8
+FP8 = mybir.dt.float8_e4m3fn
+FP8X4 = mybir.dt.float8_e4m3fn_x4
+ALU = mybir.AluOpType
+ACT = mybir.ActivationFunctionType
+
+P = 128
+GROUP = 512
+GROUPS = S // GROUP
+TILES = H * T // P
+POOL_COLS = 1280
+POOL_SPARE = 768
+WIDE_HEAD = 5
+WIDE_V = 2
+QY_LAG = 1
+KCOPY_AT = 2
+LATE_V = 0
+MM_EARLY = 0
+USE_SPARE = True
+ACT_FIRST = True
+MEAN_PSUM = True
+
+
+def tile_centred_key_capped_logits_b15_kernel(
+    tc, keys_bytes, keys_scale, keys_mean, queries, temp, cap, out_0, out_1, out_2
+):
+    nc = tc.nc
+    y_rows = out_0.rearrange("h (a m) s -> (h a) m s", m=TILES)
+    q_rows = queries.rearrange("h (a m) d -> (h a) m d", m=TILES)
+
+    with ExitStack() as ctx:
+        keep = ctx.enter_context(tc.tile_pool(name="keep", bufs=1))
+        work = ctx.enter_context(tc.tile_pool(name="work", bufs=2))
+        psum = ctx.enter_context(tc.psum_pool(name="psum", bufs=1))
+        ctx.enter_context(tc.manual_schedule())
+
+        key_bytes = {}
+
+        def load_keys(g):
+            tile = keep.tile([P, 4 * D], U8, name="key_bytes", bufs=GROUPS, align_bytes=64)
+            nc.sync.dma_start(out=tile[:], in_=keys_bytes[g * GROUP:(g + 1) * GROUP, :].rearrange("(p j) d -> p (j d)", j=4))
+            key_bytes[g] = tile
+
+        load_keys(0)
+        key_scale = keep.tile([P, GROUPS, 16], F32, name="key_scale")
+        nc.sync.dma_start(out=key_scale[:], in_=keys_scale.rearrange("(g p j) b -> p g (j b)", p=P, j=4))
+        if MEAN_PSUM:
+            mean_words = keep.tile([P, 2], F32, name="mean_words")
+            with nc.allow_non_contiguous_dma(reason="one word of the mean to a partition"):
+                nc.sync.dma_start(out=mean_words[:], in_=keys_mean.bitcast(F32).rearrange("o (h p) -> p (o h)", p=P))
+        else:
+            mean_sb = keep.tile([P, D], BF16, name="mean_sb")
+            nc.sync.dma_start(out=mean_sb[:], in_=keys_mean.rearrange("o d -> (o d)").partition_broadcast(P))
+        q_raw = []
+        for half in range(2):
+            tile = keep.tile([P, 4, D], BF16, name="q_raw", bufs=2)
+            nc.sync.dma_start(out=tile[:], in_=q_rows[:, 4 * half:4 * half + 4, :])
+            q_raw.append(tile)
+            if half == 0:
+                load_keys(1)
+        cap_all = keep.tile([P, H], BF16, name="cap_all")
+        nc.sync.dma_start(out=cap_all[:], in_=cap.rearrange("h a b -> (h a b)").partition_broadcast(P))
+        temp_sb = keep.tile([P, TILES], BF16, name="temp_sb")
+        nc.sync.dma_start(out=temp_sb[:], in_=temp.rearrange("h (a m) o -> (h a) (m o)", m=TILES))
+        for g in range(2, GROUPS):
+            load_keys(g)
+
+        ident = keep.tile([P, P], F32, name="ident")
+        make_identity(nc, ident[:])
+        head_mask = keep.tile([P, H], F32, name="head_mask")
+        nc.gpsimd.memset(head_mask[:], 1.0)
+        nc.gpsimd.affine_select(out=head_mask[:], in_=head_mask[:], pattern=[[-8, H]], compare_op=ALU.is_ge,
+                                fill=0.0, base=0, channel_multiplier=1)
+        nc.gpsimd.affine_select(out=head_mask[:], in_=head_mask[:], pattern=[[8, H]], compare_op=ALU.is_ge,
+                                fill=0.0, base=7, channel_multiplier=-1)
+
+        if MEAN_PSUM:
+            mean_bank = psum.tile([P, 2, P], F32, name="mean_bank")
+            for h in range(2):
+                nc.tensor.transpose(mean_bank[:, h, :], mean_words[:, h:h + 1].to_broadcast([P, P]), ident[:])
+            mean_row = mean_bank[:].rearrange("p h w -> p (h w)").bitcast(BF16)
+        else:
+            mean_row = mean_sb[:]
+
+        def turn_bank():
+            return psum.tile([P, 4, P], F32, name="turn", bufs=4)
+
+        def copy_on(vector, out, in_):
+            if vector:
+                nc.vector.tensor_copy(out=out, in_=in_)
+            else:
+                nc.scalar.copy(out=out, in_=in_)
+
+        wide, value, kbank, kgroup, kq = {}, {}, {}, {}, {}
+
+        def widen(g, half, vector=False):
+            tile = work.tile([P, 2 * D], BF16, name="wide", bufs=10)
+            codes = key_bytes[g][:, half * 2 * D:(half + 1) * 2 * D].bitcast(FP8)
+            if ACT_FIRST and (g, half) == (0, 1):
+                nc.scalar.activation(out=tile[:], in_=codes, func=ACT.Copy)
+            else:
+                copy_on(vector, tile[:], codes)
+            wide[g, half] = tile
+
+        def dequantise(g, half):
+            tile = work.tile([P, 2 * D], BF16, name="value", bufs=4)
+            for jj in range(2):
+                for b in range(4):
+                    cols = slice(jj * D + b * B, jj * D + (b + 1) * B)
+                    col = 4 * (2 * half + jj) + b
+                    nc.vector.scalar_tensor_tensor(
+                        out=tile[:, cols], in0=wide[g, half][:, cols], scalar=key_scale[:, g, col:col + 1],
+                        in1=mean_row[:, b * B:(b + 1) * B], op0=ALU.mult, op1=ALU.add)
+            value[g, half] = tile
+
+        def turn_rows(words):
+            bank = turn_bank()
+            for r in range(2):
+                for u in range(2):
+                    nc.tensor.transpose(bank[:, 2 * r + u, :], words[:, r * 256 + u:(r + 1) * 256:2], ident[:])
+            return bank
+
+        def turn_keys(g, half):
+            kbank[g, half] = turn_rows(value[g, half][:].bitcast(F32))
+
+        def copy_keys(g, half, vector=False):
+            if half == 0:
+                kgroup[g] = work.tile([P, GROUP * 4], BF16, name="kgroup", bufs=2, align_bytes=64)
+            out = kgroup[g][:].bitcast(F32).rearrange("c (p w) -> c p w", w=8)[:, :, 4 * half:4 * half + 4]
+            copy_on(vector, out, kbank[g, half][:].rearrange("c w p -> c p w"))
+
+        def quantise_keys(g):
+            codes = work.tile([P, GROUP], U32, name="kcodes", bufs=3, align_bytes=64)
+            scales = work.tile([P, GROUP], U8, name="kscales", bufs=3, align_bytes=64)
+            nc.vector.quantize_mx(out=codes[:].bitcast(FP8X4), scales=scales[:], in_=kgroup[g][:])
+            kq[g] = (codes, scales)
+
+        qbank, qgroup, qq = {}, {}, {}
+
+        def turn_queries(pair):
+            words = q_raw[pair // 2][:].rearrange("p m d -> p (m d)").bitcast(F32)
+            qbank[pair] = turn_rows(words[:, (pair % 2) * 512:(pair % 2 + 1) * 512])
+
+        def copy_queries(pair, vector=False):
+            if pair % 2 == 0:
+                qgroup[pair // 2] = keep.tile([P, 4 * P * 4], BF16, name="qgroup", bufs=2, align_bytes=64)
+            out = qgroup[pair // 2][:].bitcast(F32)[:, (pair % 2) * 512:(pair % 2 + 1) * 512]
+            copy_on(vector, out.rearrange("c (r p u) -> c r p u", r=2, u=2),
+                    qbank[pair][:].rearrange("c (r u) p -> c r p u", u=2))
+
+        def quantise_queries(half):
+            codes = keep.tile([P, 4 * P], U32, name="qcodes", bufs=2, align_bytes=64)
+            scales = keep.tile([P, 4 * P], U8, name="qscales", bufs=2, align_bytes=64)
+            nc.vector.quantize_mx(out=codes[:].bitcast(FP8X4), scales=scales[:], in_=qgroup[half][:])
+            qq[half] = (codes, scales)
+
+        consts = {}
+
+        def make_constants():
+            picked = keep.tile([P, H], F32, name="picked")
+            nc.vector.tensor_tensor(out=picked[:], in0=cap_all[:], in1=head_mask[:], op=ALU.mult)
+            cap_col = keep.tile([P, 1], F32, name="cap_col")
+            nc.vector.tensor_reduce(out=cap_col[:], in_=picked[:], op=ALU.add, axis=mybir.AxisListType.X)
+            inv_cap = keep.tile([P, 1], F32, name="inv_cap")
+            nc.vector.reciprocal(out=inv_cap[:], in_=cap_col[:])
+            slope = keep.tile([P, TILES], F32, name="slope")
+            nc.vector.tensor_scalar(out=slope[:], in0=temp_sb[:], scalar1=inv_cap[:], scalar2=None, op0=ALU.mult)
+            consts["cap"] = cap_col
+            consts["slope"] = slope
+
+        raw, ty = {}, {}
+
+        def multiply(g, m):
+            bank = psum.tile([P, GROUP], F32, name="raw", bufs=3)
+            cols = slice((m % 4) * P, (m % 4 + 1) * P)
+            nc.tensor.matmul_mx(out=bank[:], lhsT=qq[m // 4][0][:, cols].bitcast(FP8X4), lhsT_scale=qq[m // 4][1][:, cols],
+                                rhs=kq[g][0][:].bitcast(FP8X4), rhs_scale=kq[g][1][:], start=True, stop=True)
+            raw[g, m] = bank
+
+        def squash(g, m):
+            if m == 0:
+                ty[g] = work.tile([P, TILES, GROUP], F32, name="ty", bufs=4)
+            nc.scalar.activation(out=ty[g][:, m, :], in_=raw[g, m][:], func=ACT.Tanh, scale=consts["slope"][:, m:m + 1])
+
+        rounded, ybank, ygroup, yscales = {}, {}, {}, {}
+
+        def round_y(g, m0, m1):
+            tile = work.tile([P, 2, m1 - m0, 256], BF16, name="rounded", bufs=3)
+            nc.vector.tensor_scalar(
+                out=tile[:].rearrange("q u m (p e) -> q u (m p) e", e=2),
+                in0=ty[g][:, m0:m1, :].rearrange("q m (p u e) -> q u (m p) e", u=2, e=2),
+                scalar1=consts["cap"][:], scalar2=None, op0=ALU.mult)
+            for m in range(m0, m1):
+                rounded[g, m] = (tile, m - m0)
+
+        def round_scaled(g, m0, m1):
+            tile = work.tile([P, 2, m1 - m0, 256], BF16, name="rounded", bufs=3)
+            nc.vector.tensor_copy(
+                out=tile[:].rearrange("q u m (p e) -> q u (m p) e", e=2),
+                in_=ty[g][:, m0:m1, :].rearrange("q m (p u e) -> q u (m p) e", u=2, e=2))
+            for m in range(m0, m1):
+                rounded[g, m] = (tile, m - m0)
+
+        def scale_y(g, c0, c1, engine):
+            view = ty[g][:].rearrange("q m s -> q (m s)")[:, c0:c1]
+            if engine is nc.scalar:
+                engine.activation(out=view, in_=view, func=ACT.Copy, scale=consts["cap"][:])
+            elif engine is nc.gpsimd:
+                engine.tensor_scalar(out=view, in0=view, scalar1=consts["cap"][:], scalar2=1.0, op0=ALU.mult, op1=ALU.mult)
+            else:
+                engine.tensor_scalar(out=view, in0=view, scalar1=consts["cap"][:], scalar2=None, op0=ALU.mult)
+
+        def store_y(g, m0, m1):
+            nc.sync.dma_start(out=y_rows[:, m0:m1, g * GROUP:(g + 1) * GROUP], in_=ty[g][:, m0:m1, :])
+
+        def turn_y(g, pair):
+            bank = turn_bank()
+            for r in range(2):
+                tile, at = rounded[g, 2 * pair + r]
+                for u in range(2):
+                    nc.tensor.transpose(bank[:, 2 * r + u, :], tile[:, u, at, :].bitcast(F32), ident[:])
+            ybank[g, pair] = bank
+
+        def copy_y(g, pair, vector):
+            if g not in ygroup:
+                ygroup[g] = work.tile([P, H * T * 4], BF16, name="ygroup", bufs=2, align_bytes=64)
+            out = ygroup[g][:].bitcast(F32).rearrange("p (q w) -> p q w", w=2 * TILES)[:, :, 4 * pair:4 * pair + 4]
+            copy_on(vector, out, ybank[g, pair][:].rearrange("p w q -> p q w"))
+
+        batches = [(0, 4), (4, 7), (7, 8)]
+
+        def quantise_y(g):
+            first, last = [b for b in batches if b[0] <= g < b[1]][0]
+            if g == first:
+                yscales[first] = keep.tile([P, last - first, H * T], U8, name="yscales", bufs=3, align_bytes=64)
+            codes = work.tile([P, H * T], U32, name="ycodes", bufs=3, align_bytes=64)
+            nc.vector.quantize_mx(out=codes[:].bitcast(FP8X4), scales=yscales[first][:, g - first, :], in_=ygroup[g][:])
+            nc.sync.dma_start(out=out_1[g].rearrange("p m t -> p (m t)").bitcast(I32), in_=codes[:].bitcast(I32))
+            if g == last - 1:
+                for quad in range(4):
+                    nc.sync.dma_start(
+                        out=out_2[first:last, 4 * quad:4 * quad + 4, :].rearrange("g r m -> r g m").bitcast(I32),
+                        in_=yscales[first][32 * quad:32 * quad + 4, :, :].bitcast(I32))
+
+        widen(0, 0, True)
+        widen(0, 1)
+        dequantise(0, 0)
+        dequantise(0, 1)
+        turn_queries(0)
+        turn_queries(1)
+        turn_keys(0, 0)
+        turn_keys(0, 1)
+        copy_queries(0)
+        copy_queries(1)
+        widen(1, 0)
+        copy_keys(0, 0)
+        copy_keys(0, 1)
+        make_constants()
+        quantise_queries(0)
+        turn_queries(2)
+        turn_queries(3)
+        quantise_keys(0)
+        dequantise(1, 0)
+        copy_queries(2)
+        copy_queries(3)
+        for m in range(3):
+            multiply(0, m)
+        turn_keys(1, 0)
+        for c in range(3, WIDE_HEAD):
+            widen(c // 2, c % 2)
+        quantise_queries(1)
+        widened = WIDE_HEAD
+        halves = 2 * GROUPS
+        unit = 4 * GROUP
+        quantised = 0
+
+        for h in range(halves + 1):
+            g, m0 = h // 2, 4 * (h % 2)
+            c = h + 3
+            has_k, has_t, has_y = c < halves, h < halves, h > 0
+            yg, y0 = (h - 1) // 2, 4 * ((h - 1) % 2)
+            c0 = y0 * GROUP
+            need_wide = widened < min(c + 2, halves)
+            spare = USE_SPARE and not need_wide
+            pool = (POOL_SPARE if spare else POOL_COLS) if has_k else 0
+            on_v = (0 if spare else 1) if has_k else LATE_V
+            if has_y and has_k:
+                round_y(yg, y0, y0 + 4)
+                if pool:
+                    scale_y(yg, c0, c0 + pool, nc.gpsimd)
+            elif has_y:
+                for i in range(2):
+                    scale_y(yg, c0 + i * unit // 2, c0 + (i + 1) * unit // 2, nc.vector)
+                store_y(yg, y0, y0 + 4)
+                for i in range(2):
+                    round_scaled(yg, y0 + 2 * i, y0 + 2 * i + 2)
+            nxt = [((h + 1) // 2, 4 * ((h + 1) % 2) + i) for i in range(3)] if h + 1 < halves else []
+            for i in range(4):
+                if i == KCOPY_AT and c - 1 < halves:
+                    copy_keys((c - 1) // 2, (c - 1) % 2)
+                if has_t:
+                    squash(g, m0 + i)
+                if i == 0:
+                    if has_t:
+                        multiply(g, m0 + 3)
+                    if has_y:
+                        turn_y(yg, y0 // 2)
+                        turn_y(yg, y0 // 2 + 1)
+            if h % 2 == 0:
+                for gm in nxt[:MM_EARLY]:
+                    multiply(*gm)
+            if has_k:
+                dequantise(c // 2, c % 2)
+                turn_keys(c // 2, c % 2)
+            if has_y:
+                if on_v:
+                    copy_y(yg, y0 // 2, True)
+                if has_k and pool < unit:
+                    scale_y(yg, c0 + pool, c0 + unit, nc.vector)
+                if has_k:
+                    store_y(yg, y0, y0 + 4)
+            else:
+                for i in range(WIDE_V):
+                    widen(widened // 2, widened % 2, True)
+                    widened = widened + 1
+            if h % 2 == 1 and g + 1 < GROUPS:
+                quantise_keys(g + 1)
+            for gm in nxt[MM_EARLY if h % 2 == 0 else 0:]:
+                multiply(*gm)
+            lag = QY_LAG if has_k else 1
+            if 2 * quantised + 2 + lag <= h:
+                quantise_y(quantised)
+                quantised = quantised + 1
+            if has_y and not on_v:
+                copy_y(yg, y0 // 2, False)
+            if widened < min(c + 2, halves):
+                widen(widened // 2, widened % 2)
+                widened = widened + 1
+            if has_y:
+                copy_y(yg, y0 // 2 + 1, on_v > 1)
+        for g in range(quantised, GROUPS):
+            quantise_y(g)

@@ -20,15 +20,22 @@ P = 128
 GROUP = 512
 GROUPS = S // GROUP
 TILES = H * T // P
-POOL_COLS = 1280
-POOL_SPARE = 768
+POOL_COLS = 1536
 WIDE_HEAD = 5
-WIDE_V = 2
-QY_LAG = 1
-KCOPY_AT = 2
+WIDE_V = 1
+HEAD_V = 0
+H1_POOL = 0
+WARM_N = 256
+WARM_FROM = 0
+WARM_TO = 64
+TA = 0
+TB = 2
+TK = 2
+TA2 = 1
+TB2 = 1
 LATE_V = 0
-MM_EARLY = 0
-USE_SPARE = True
+TAIL_S = 1
+LATE_POOL = 0
 ACT_FIRST = True
 MEAN_PSUM = True
 
@@ -63,17 +70,23 @@ def tile_centred_key_capped_logits_b15_kernel(
         else:
             mean_sb = keep.tile([P, D], BF16, name="mean_sb")
             nc.sync.dma_start(out=mean_sb[:], in_=keys_mean.rearrange("o d -> (o d)").partition_broadcast(P))
-        q_raw = []
-        for half in range(2):
-            tile = keep.tile([P, 4, D], BF16, name="q_raw", bufs=2)
-            nc.sync.dma_start(out=tile[:], in_=q_rows[:, 4 * half:4 * half + 4, :])
-            q_raw.append(tile)
-            if half == 0:
-                load_keys(1)
+        q_raw = {}
+
+        def load_queries(first, last):
+            tile = keep.tile([P, 2 * (last - first), D], BF16, name="q_raw", bufs=3)
+            nc.sync.dma_start(out=tile[:], in_=q_rows[:, 2 * first:2 * last, :])
+            words = tile[:].rearrange("p m d -> p (m d)").bitcast(F32)
+            for pair in range(first, last):
+                q_raw[pair] = words[:, (pair - first) * 512:(pair - first + 1) * 512]
+
+        load_queries(0, 1)
         cap_all = keep.tile([P, H], BF16, name="cap_all")
         nc.sync.dma_start(out=cap_all[:], in_=cap.rearrange("h a b -> (h a b)").partition_broadcast(P))
         temp_sb = keep.tile([P, TILES], BF16, name="temp_sb")
         nc.sync.dma_start(out=temp_sb[:], in_=temp.rearrange("h (a m) o -> (h a) (m o)", m=TILES))
+        load_queries(1, 2)
+        load_keys(1)
+        load_queries(2, 4)
         for g in range(2, GROUPS):
             load_keys(g)
 
@@ -150,42 +163,34 @@ def tile_centred_key_capped_logits_b15_kernel(
         qbank, qgroup, qq = {}, {}, {}
 
         def turn_queries(pair):
-            words = q_raw[pair // 2][:].rearrange("p m d -> p (m d)").bitcast(F32)
-            qbank[pair] = turn_rows(words[:, (pair % 2) * 512:(pair % 2 + 1) * 512])
+            qbank[pair] = turn_rows(q_raw[pair])
 
         def copy_queries(pair, vector=False):
-            if pair % 2 == 0:
-                qgroup[pair // 2] = keep.tile([P, 4 * P * 4], BF16, name="qgroup", bufs=2, align_bytes=64)
-            out = qgroup[pair // 2][:].bitcast(F32)[:, (pair % 2) * 512:(pair % 2 + 1) * 512]
-            copy_on(vector, out.rearrange("c (r p u) -> c r p u", r=2, u=2),
+            qgroup[pair] = keep.tile([P, 2 * P * 4], BF16, name="qgroup", bufs=4, align_bytes=64)
+            copy_on(vector, qgroup[pair][:].bitcast(F32).rearrange("c (r p u) -> c r p u", r=2, u=2),
                     qbank[pair][:].rearrange("c (r u) p -> c r p u", u=2))
 
-        def quantise_queries(half):
-            codes = keep.tile([P, 4 * P], U32, name="qcodes", bufs=2, align_bytes=64)
-            scales = keep.tile([P, 4 * P], U8, name="qscales", bufs=2, align_bytes=64)
-            nc.vector.quantize_mx(out=codes[:].bitcast(FP8X4), scales=scales[:], in_=qgroup[half][:])
-            qq[half] = (codes, scales)
+        def quantise_queries(pair):
+            codes = keep.tile([P, 2 * P], U32, name="qcodes", bufs=4, align_bytes=64)
+            scales = keep.tile([P, 2 * P], U8, name="qscales", bufs=4, align_bytes=64)
+            nc.vector.quantize_mx(out=codes[:].bitcast(FP8X4), scales=scales[:], in_=qgroup[pair][:])
+            qq[pair] = (codes, scales)
 
-        consts = {}
-
-        def make_constants():
-            picked = keep.tile([P, H], F32, name="picked")
-            nc.vector.tensor_tensor(out=picked[:], in0=cap_all[:], in1=head_mask[:], op=ALU.mult)
-            cap_col = keep.tile([P, 1], F32, name="cap_col")
-            nc.vector.tensor_reduce(out=cap_col[:], in_=picked[:], op=ALU.add, axis=mybir.AxisListType.X)
-            inv_cap = keep.tile([P, 1], F32, name="inv_cap")
-            nc.vector.reciprocal(out=inv_cap[:], in_=cap_col[:])
-            slope = keep.tile([P, TILES], F32, name="slope")
-            nc.vector.tensor_scalar(out=slope[:], in0=temp_sb[:], scalar1=inv_cap[:], scalar2=None, op0=ALU.mult)
-            consts["cap"] = cap_col
-            consts["slope"] = slope
+        picked = keep.tile([P, H], F32, name="picked")
+        cap_col = keep.tile([P, 1], F32, name="cap_col")
+        inv_cap = keep.tile([P, 1], F32, name="inv_cap")
+        slope = keep.tile([P, TILES], F32, name="slope")
+        consts = {"cap": cap_col, "slope": slope}
 
         raw, ty = {}, {}
 
         def multiply(g, m):
             bank = psum.tile([P, GROUP], F32, name="raw", bufs=3)
-            cols = slice((m % 4) * P, (m % 4 + 1) * P)
-            nc.tensor.matmul_mx(out=bank[:], lhsT=qq[m // 4][0][:, cols].bitcast(FP8X4), lhsT_scale=qq[m // 4][1][:, cols],
+            cols = slice((m % 2) * P, (m % 2 + 1) * P)
+            if WARM_N and WARM_FROM <= TILES * g + m < WARM_TO:
+                nc.tensor.matmul_mx(out=bank[:, 0:WARM_N], lhsT=qq[m // 2][0][:, cols].bitcast(FP8X4), lhsT_scale=qq[m // 2][1][:, cols],
+                                    rhs=kq[g][0][:, 0:WARM_N].bitcast(FP8X4), rhs_scale=kq[g][1][:, 0:WARM_N], start=True, stop=True)
+            nc.tensor.matmul_mx(out=bank[:], lhsT=qq[m // 2][0][:, cols].bitcast(FP8X4), lhsT_scale=qq[m // 2][1][:, cols],
                                 rhs=kq[g][0][:].bitcast(FP8X4), rhs_scale=kq[g][1][:], start=True, stop=True)
             raw[g, m] = bank
 
@@ -197,7 +202,7 @@ def tile_centred_key_capped_logits_b15_kernel(
         rounded, ybank, ygroup, yscales = {}, {}, {}, {}
 
         def round_y(g, m0, m1):
-            tile = work.tile([P, 2, m1 - m0, 256], BF16, name="rounded", bufs=3)
+            tile = work.tile([P, 2, m1 - m0, 256], BF16, name="rounded", bufs=4)
             nc.vector.tensor_scalar(
                 out=tile[:].rearrange("q u m (p e) -> q u (m p) e", e=2),
                 in0=ty[g][:, m0:m1, :].rearrange("q m (p u e) -> q u (m p) e", u=2, e=2),
@@ -206,7 +211,7 @@ def tile_centred_key_capped_logits_b15_kernel(
                 rounded[g, m] = (tile, m - m0)
 
         def round_scaled(g, m0, m1):
-            tile = work.tile([P, 2, m1 - m0, 256], BF16, name="rounded", bufs=3)
+            tile = work.tile([P, 2, m1 - m0, 256], BF16, name="rounded", bufs=4)
             nc.vector.tensor_copy(
                 out=tile[:].rearrange("q u m (p e) -> q u (m p) e", e=2),
                 in_=ty[g][:, m0:m1, :].rearrange("q m (p u e) -> q u (m p) e", u=2, e=2))
@@ -239,7 +244,18 @@ def tile_centred_key_capped_logits_b15_kernel(
             out = ygroup[g][:].bitcast(F32).rearrange("p (q w) -> p q w", w=2 * TILES)[:, :, 4 * pair:4 * pair + 4]
             copy_on(vector, out, ybank[g, pair][:].rearrange("p w q -> p q w"))
 
-        batches = [(0, 4), (4, 7), (7, 8)]
+        def turn_one(g, m):
+            bank = turn_bank()
+            tile, at = rounded[g, m]
+            for u in range(2):
+                nc.tensor.transpose(bank[:, u, :], tile[:, u, at, :].bitcast(F32), ident[:])
+            ybank[g, m, 1] = bank
+
+        def copy_one(g, m, vector):
+            out = ygroup[g][:].bitcast(F32).rearrange("p (q w) -> p q w", w=2 * TILES)[:, :, 2 * m:2 * m + 2]
+            copy_on(vector, out, ybank[g, m, 1][:, 0:2, :].rearrange("p w q -> p q w"))
+
+        batches = [(0, 3), (3, 6), (6, 8)]
 
         def quantise_y(g):
             first, last = [b for b in batches if b[0] <= g < b[1]][0]
@@ -257,98 +273,125 @@ def tile_centred_key_capped_logits_b15_kernel(
         widen(0, 0, True)
         widen(0, 1)
         dequantise(0, 0)
+        nc.vector.tensor_tensor(out=picked[:], in0=cap_all[:], in1=head_mask[:], op=ALU.mult)
         dequantise(0, 1)
+        nc.vector.tensor_reduce(out=cap_col[:], in_=picked[:], op=ALU.add, axis=mybir.AxisListType.X)
         turn_queries(0)
-        turn_queries(1)
         turn_keys(0, 0)
         turn_keys(0, 1)
+        turn_queries(1)
         copy_queries(0)
-        copy_queries(1)
         widen(1, 0)
         copy_keys(0, 0)
+        widen(1, 1)
         copy_keys(0, 1)
-        make_constants()
         quantise_queries(0)
+        nc.vector.reciprocal(out=inv_cap[:], in_=cap_col[:])
+        dequantise(1, 0)
+        nc.vector.tensor_scalar(out=slope[:], in0=temp_sb[:], scalar1=inv_cap[:], scalar2=None, op0=ALU.mult)
+        quantise_keys(0)
+        copy_queries(1)
+        widen(2, 0)
+        multiply(0, 0)
+        multiply(0, 1)
+        quantise_queries(1)
+        multiply(0, 2)
         turn_queries(2)
         turn_queries(3)
-        quantise_keys(0)
-        dequantise(1, 0)
-        copy_queries(2)
-        copy_queries(3)
-        for m in range(3):
-            multiply(0, m)
+        dequantise(1, 1)
+        squash(0, 0)
+        multiply(0, 3)
+        squash(0, 1)
         turn_keys(1, 0)
-        for c in range(3, WIDE_HEAD):
-            widen(c // 2, c % 2)
-        quantise_queries(1)
-        widened = WIDE_HEAD
+        dequantise(2, 0)
+        copy_queries(2)
+        quantise_queries(2)
+        multiply(0, 4)
+        squash(0, 2)
+        turn_keys(1, 1)
+        copy_queries(3)
+        widen(2, 1, True)
+        quantise_queries(3)
+        multiply(0, 5)
+        squash(0, 3)
+        copy_keys(1, 0, HEAD_V > 0)
+        multiply(0, 6)
+        turn_keys(2, 0)
+        copy_keys(1, 1, HEAD_V > 1)
+        widened = 5 + WIDE_V
         halves = 2 * GROUPS
         unit = 4 * GROUP
-        quantised = 0
+        owed = []
 
-        for h in range(halves + 1):
+        for h in range(1, halves):
             g, m0 = h // 2, 4 * (h % 2)
-            c = h + 3
-            has_k, has_t, has_y = c < halves, h < halves, h > 0
+            c = h + 4
+            has_k = c < halves
             yg, y0 = (h - 1) // 2, 4 * ((h - 1) % 2)
             c0 = y0 * GROUP
-            need_wide = widened < min(c + 2, halves)
-            spare = USE_SPARE and not need_wide
-            pool = (POOL_SPARE if spare else POOL_COLS) if has_k else 0
-            on_v = (0 if spare else 1) if has_k else LATE_V
-            if has_y and has_k:
-                round_y(yg, y0, y0 + 4)
-                if pool:
-                    scale_y(yg, c0, c0 + pool, nc.gpsimd)
-            elif has_y:
-                for i in range(2):
-                    scale_y(yg, c0 + i * unit // 2, c0 + (i + 1) * unit // 2, nc.vector)
-                store_y(yg, y0, y0 + 4)
-                for i in range(2):
-                    round_scaled(yg, y0 + 2 * i, y0 + 2 * i + 2)
-            nxt = [((h + 1) // 2, 4 * ((h + 1) % 2) + i) for i in range(3)] if h + 1 < halves else []
-            for i in range(4):
-                if i == KCOPY_AT and c - 1 < halves:
-                    copy_keys((c - 1) // 2, (c - 1) % 2)
-                if has_t:
-                    squash(g, m0 + i)
-                if i == 0:
-                    if has_t:
-                        multiply(g, m0 + 3)
-                    if has_y:
-                        turn_y(yg, y0 // 2)
-                        turn_y(yg, y0 // 2 + 1)
-            if h % 2 == 0:
-                for gm in nxt[:MM_EARLY]:
-                    multiply(*gm)
+            on_v = has_k or (LATE_V and h % LATE_V == LATE_V - 1)
+            pool = (POOL_COLS if h > 1 else H1_POOL) if has_k else 0
+            first = (pool + GROUP - 1) // GROUP if pool else 2
+            ahead = [((h + (i + 3) // 4) // 2, (m0 + i + 3) % TILES) for i in range(4)]
+            round_y(yg, y0, y0 + first)
+            if pool:
+                scale_y(yg, c0, c0 + pool, nc.gpsimd)
+            round_y(yg, y0 + first, y0 + 4)
+            if h == 1:
+                quantise_keys(1)
             if has_k:
                 dequantise(c // 2, c % 2)
-                turn_keys(c // 2, c % 2)
-            if has_y:
-                if on_v:
-                    copy_y(yg, y0 // 2, True)
-                if has_k and pool < unit:
-                    scale_y(yg, c0 + pool, c0 + unit, nc.vector)
-                if has_k:
-                    store_y(yg, y0, y0 + 4)
             else:
-                for i in range(WIDE_V):
-                    widen(widened // 2, widened % 2, True)
-                    widened = widened + 1
-            if h % 2 == 1 and g + 1 < GROUPS:
-                quantise_keys(g + 1)
-            for gm in nxt[MM_EARLY if h % 2 == 0 else 0:]:
-                multiply(*gm)
-            lag = QY_LAG if has_k else 1
-            if 2 * quantised + 2 + lag <= h:
-                quantise_y(quantised)
-                quantised = quantised + 1
-            if has_y and not on_v:
-                copy_y(yg, y0 // 2, False)
-            if widened < min(c + 2, halves):
-                widen(widened // 2, widened % 2)
-                widened = widened + 1
-            if has_y:
-                copy_y(yg, y0 // 2 + 1, on_v > 1)
-        for g in range(quantised, GROUPS):
-            quantise_y(g)
+                scale_y(yg, c0, c0 + unit, nc.vector)
+                store_y(yg, y0, y0 + 4)
+            for i in range(4):
+                squash(g, m0 + i)
+                if ahead[i][0] < GROUPS:
+                    multiply(*ahead[i])
+                if i == (TA if has_k else TA2):
+                    turn_y(yg, y0 // 2)
+                if i == (TB if has_k else TB2):
+                    turn_y(yg, y0 // 2 + 1)
+                if has_k and i == TK:
+                    turn_keys(c // 2, c % 2)
+                if i == 0 and owed:
+                    copy_y(*owed[0], False)
+                    owed = owed[1:]
+                if i == 1 and c - 1 < halves:
+                    copy_keys((c - 1) // 2, (c - 1) % 2)
+                if i == 1 and owed:
+                    copy_y(*owed[0], False)
+                    owed = owed[1:]
+                if i == 2:
+                    if has_k:
+                        copy_y(yg, y0 // 2, True)
+                        scale_y(yg, c0 + pool, c0 + unit, nc.vector)
+                        store_y(yg, y0, y0 + 4)
+                    if widened < min(c + 2, halves):
+                        widen(widened // 2, widened % 2)
+                        widened = widened + 1
+                    if h % 2 == 0 and g + 1 < GROUPS:
+                        quantise_keys(g + 1)
+                    if h % 2 == 1 and g > 0:
+                        quantise_y(g - 1)
+                    if on_v and not has_k:
+                        copy_y(yg, y0 // 2, True)
+            owed = owed + ([] if on_v else [(yg, y0 // 2)]) + [(yg, y0 // 2 + 1)]
+        g = GROUPS - 1
+        round_y(g, 4, 6)
+        for pair in owed:
+            copy_y(*pair, False)
+        turn_y(g, 2)
+        round_y(g, 6, 7)
+        turn_one(g, 6)
+        round_y(g, 7, 8)
+        turn_one(g, 7)
+        scale_y(g, 4 * GROUP, (8 - TAIL_S) * GROUP, nc.vector)
+        store_y(g, 4, 8 - TAIL_S)
+        copy_y(g, 2, False)
+        copy_one(g, 6, False)
+        copy_one(g, 7, False)
+        if TAIL_S:
+            scale_y(g, (8 - TAIL_S) * GROUP, 8 * GROUP, nc.scalar)
+            store_y(g, 8 - TAIL_S, 8)
+        quantise_y(g)

@@ -21,21 +21,23 @@ GROUP = 512
 GROUPS = S // GROUP
 TILES = H * T // P
 POOL_COLS = 1536
-WIDE_HEAD = 5
-WIDE_V = 1
-HEAD_V = 0
 H1_POOL = 0
+HEAD_V = 0
 WARM_N = 256
-WARM_FROM = 0
+WARM_FROM = 1
 WARM_TO = 64
-TA = 0
-TB = 2
+LS = 1
+LV = 1
+LATE_POOL = 512
+STEADY_S = 0
+AHEAD = 3
+TAIL_S = 0
+KSLOT = 1
+BATCHES = [(0, 3), (3, 8)]
+CAST_V = 0
+TAIL_V = (30,)
+TAIL_AT = 0
 TK = 2
-TA2 = 1
-TB2 = 1
-LATE_V = 0
-TAIL_S = 1
-LATE_POOL = 0
 ACT_FIRST = True
 MEAN_PSUM = True
 
@@ -80,12 +82,12 @@ def tile_centred_key_capped_logits_b15_kernel(
                 q_raw[pair] = words[:, (pair - first) * 512:(pair - first + 1) * 512]
 
         load_queries(0, 1)
+        load_keys(1)
         cap_all = keep.tile([P, H], BF16, name="cap_all")
         nc.sync.dma_start(out=cap_all[:], in_=cap.rearrange("h a b -> (h a b)").partition_broadcast(P))
         temp_sb = keep.tile([P, TILES], BF16, name="temp_sb")
         nc.sync.dma_start(out=temp_sb[:], in_=temp.rearrange("h (a m) o -> (h a) (m o)", m=TILES))
         load_queries(1, 2)
-        load_keys(1)
         load_queries(2, 4)
         for g in range(2, GROUPS):
             load_keys(g)
@@ -118,14 +120,15 @@ def tile_centred_key_capped_logits_b15_kernel(
 
         wide, value, kbank, kgroup, kq = {}, {}, {}, {}, {}
 
-        def widen(g, half, vector=False):
-            tile = work.tile([P, 2 * D], BF16, name="wide", bufs=10)
-            codes = key_bytes[g][:, half * 2 * D:(half + 1) * 2 * D].bitcast(FP8)
+        def widen(g, half, vector=False, parts=(0, 1)):
+            if parts[0] == 0:
+                wide[g, half] = work.tile([P, 2 * D], BF16, name="wide", bufs=5)
+            lo, hi = parts[0] * D, (parts[-1] + 1) * D
+            codes = key_bytes[g][:, half * 2 * D + lo:half * 2 * D + hi].bitcast(FP8)
             if ACT_FIRST and (g, half) == (0, 1):
-                nc.scalar.activation(out=tile[:], in_=codes, func=ACT.Copy)
+                nc.scalar.activation(out=wide[g, half][:, lo:hi], in_=codes, func=ACT.Copy)
             else:
-                copy_on(vector, tile[:], codes)
-            wide[g, half] = tile
+                copy_on(vector, wide[g, half][:, lo:hi], codes)
 
         def dequantise(g, half):
             tile = work.tile([P, 2 * D], BF16, name="value", bufs=4)
@@ -202,21 +205,12 @@ def tile_centred_key_capped_logits_b15_kernel(
         rounded, ybank, ygroup, yscales = {}, {}, {}, {}
 
         def round_y(g, m0, m1):
-            tile = work.tile([P, 2, m1 - m0, 256], BF16, name="rounded", bufs=4)
+            if m0 % 4 == 0:
+                rounded[g, m0 // 4] = work.tile([P, 2, 4, 256], BF16, name="rounded", bufs=8)
             nc.vector.tensor_scalar(
-                out=tile[:].rearrange("q u m (p e) -> q u (m p) e", e=2),
+                out=rounded[g, m0 // 4][:, :, m0 % 4:m0 % 4 + m1 - m0, :].rearrange("q u m (p e) -> q u (m p) e", e=2),
                 in0=ty[g][:, m0:m1, :].rearrange("q m (p u e) -> q u (m p) e", u=2, e=2),
                 scalar1=consts["cap"][:], scalar2=None, op0=ALU.mult)
-            for m in range(m0, m1):
-                rounded[g, m] = (tile, m - m0)
-
-        def round_scaled(g, m0, m1):
-            tile = work.tile([P, 2, m1 - m0, 256], BF16, name="rounded", bufs=4)
-            nc.vector.tensor_copy(
-                out=tile[:].rearrange("q u m (p e) -> q u (m p) e", e=2),
-                in_=ty[g][:, m0:m1, :].rearrange("q m (p u e) -> q u (m p) e", u=2, e=2))
-            for m in range(m0, m1):
-                rounded[g, m] = (tile, m - m0)
 
         def scale_y(g, c0, c1, engine):
             view = ty[g][:].rearrange("q m s -> q (m s)")[:, c0:c1]
@@ -233,35 +227,24 @@ def tile_centred_key_capped_logits_b15_kernel(
         def turn_y(g, pair):
             bank = turn_bank()
             for r in range(2):
-                tile, at = rounded[g, 2 * pair + r]
+                tile, at = rounded[g, pair // 2], 2 * (pair % 2) + r
                 for u in range(2):
                     nc.tensor.transpose(bank[:, 2 * r + u, :], tile[:, u, at, :].bitcast(F32), ident[:])
             ybank[g, pair] = bank
 
         def copy_y(g, pair, vector):
             if g not in ygroup:
-                ygroup[g] = work.tile([P, H * T * 4], BF16, name="ygroup", bufs=2, align_bytes=64)
+                ygroup[g] = work.tile([P, H * T * 4], BF16, name="ygroup", bufs=3, align_bytes=64)
             out = ygroup[g][:].bitcast(F32).rearrange("p (q w) -> p q w", w=2 * TILES)[:, :, 4 * pair:4 * pair + 4]
             copy_on(vector, out, ybank[g, pair][:].rearrange("p w q -> p q w"))
 
-        def turn_one(g, m):
-            bank = turn_bank()
-            tile, at = rounded[g, m]
-            for u in range(2):
-                nc.tensor.transpose(bank[:, u, :], tile[:, u, at, :].bitcast(F32), ident[:])
-            ybank[g, m, 1] = bank
-
-        def copy_one(g, m, vector):
-            out = ygroup[g][:].bitcast(F32).rearrange("p (q w) -> p q w", w=2 * TILES)[:, :, 2 * m:2 * m + 2]
-            copy_on(vector, out, ybank[g, m, 1][:, 0:2, :].rearrange("p w q -> p q w"))
-
-        batches = [(0, 3), (3, 6), (6, 8)]
+        batches = BATCHES
 
         def quantise_y(g):
             first, last = [b for b in batches if b[0] <= g < b[1]][0]
             if g == first:
-                yscales[first] = keep.tile([P, last - first, H * T], U8, name="yscales", bufs=3, align_bytes=64)
-            codes = work.tile([P, H * T], U32, name="ycodes", bufs=3, align_bytes=64)
+                yscales[first] = keep.tile([P, last - first, H * T], U8, name="yscales", bufs=len(BATCHES), align_bytes=64)
+            codes = work.tile([P, H * T], U32, name="ycodes", bufs=5, align_bytes=64)
             nc.vector.quantize_mx(out=codes[:].bitcast(FP8X4), scales=yscales[first][:, g - first, :], in_=ygroup[g][:])
             nc.sync.dma_start(out=out_1[g].rearrange("p m t -> p (m t)").bitcast(I32), in_=codes[:].bitcast(I32))
             if g == last - 1:
@@ -280,10 +263,10 @@ def tile_centred_key_capped_logits_b15_kernel(
         turn_keys(0, 0)
         turn_keys(0, 1)
         turn_queries(1)
-        copy_queries(0)
         widen(1, 0)
-        copy_keys(0, 0)
+        copy_queries(0)
         widen(1, 1)
+        copy_keys(0, 0)
         copy_keys(0, 1)
         quantise_queries(0)
         nc.vector.reciprocal(out=inv_cap[:], in_=cap_col[:])
@@ -292,36 +275,53 @@ def tile_centred_key_capped_logits_b15_kernel(
         quantise_keys(0)
         copy_queries(1)
         widen(2, 0)
+        turn_queries(2)
         multiply(0, 0)
         multiply(0, 1)
         quantise_queries(1)
         multiply(0, 2)
-        turn_queries(2)
-        turn_queries(3)
         dequantise(1, 1)
+        copy_queries(2)
         squash(0, 0)
+        turn_queries(3)
         multiply(0, 3)
         squash(0, 1)
-        turn_keys(1, 0)
         dequantise(2, 0)
-        copy_queries(2)
         quantise_queries(2)
+        turn_keys(1, 0)
         multiply(0, 4)
+        copy_queries(3, True)
+        widen(2, 1, True)
         squash(0, 2)
         turn_keys(1, 1)
-        copy_queries(3)
-        widen(2, 1, True)
-        quantise_queries(3)
         multiply(0, 5)
+        quantise_queries(3)
         squash(0, 3)
         copy_keys(1, 0, HEAD_V > 0)
         multiply(0, 6)
         turn_keys(2, 0)
         copy_keys(1, 1, HEAD_V > 1)
-        widened = 5 + WIDE_V
         halves = 2 * GROUPS
         unit = 4 * GROUP
-        owed = []
+        state = {"turned": 0, "copied": 0, "quantised": 0}
+
+        def turn_next(limit):
+            n = state["turned"]
+            if n < limit and n - state["copied"] < AHEAD:
+                turn_y(n // 4, n % 4)
+                state["turned"] = n + 1
+
+        def copy_next(vector):
+            n = state["copied"]
+            if n < state["turned"]:
+                copy_y(n // 4, n % 4, vector)
+                state["copied"] = n + 1
+
+        def quantise_next():
+            g = state["quantised"]
+            if 4 * g + 4 <= state["copied"]:
+                quantise_y(g)
+                state["quantised"] = g + 1
 
         for h in range(1, halves):
             g, m0 = h // 2, 4 * (h % 2)
@@ -329,10 +329,10 @@ def tile_centred_key_capped_logits_b15_kernel(
             has_k = c < halves
             yg, y0 = (h - 1) // 2, 4 * ((h - 1) % 2)
             c0 = y0 * GROUP
-            on_v = has_k or (LATE_V and h % LATE_V == LATE_V - 1)
-            pool = (POOL_COLS if h > 1 else H1_POOL) if has_k else 0
+            pool = (POOL_COLS if h > 1 else H1_POOL) if has_k else LATE_POOL
             first = (pool + GROUP - 1) // GROUP if pool else 2
             ahead = [((h + (i + 3) // 4) // 2, (m0 + i + 3) % TILES) for i in range(4)]
+            done = state["copied"]
             round_y(yg, y0, y0 + first)
             if pool:
                 scale_y(yg, c0, c0 + pool, nc.gpsimd)
@@ -342,56 +342,61 @@ def tile_centred_key_capped_logits_b15_kernel(
             if has_k:
                 dequantise(c // 2, c % 2)
             else:
-                scale_y(yg, c0, c0 + unit, nc.vector)
+                for j in range(LV):
+                    copy_next(True)
+                scale_y(yg, c0 + pool, c0 + unit, nc.vector)
                 store_y(yg, y0, y0 + 4)
             for i in range(4):
                 squash(g, m0 + i)
                 if ahead[i][0] < GROUPS:
                     multiply(*ahead[i])
-                if i == (TA if has_k else TA2):
-                    turn_y(yg, y0 // 2)
-                if i == (TB if has_k else TB2):
-                    turn_y(yg, y0 // 2 + 1)
-                if has_k and i == TK:
-                    turn_keys(c // 2, c % 2)
-                if i == 0 and owed:
-                    copy_y(*owed[0], False)
-                    owed = owed[1:]
-                if i == 1 and c - 1 < halves:
+                if has_k:
+                    if i == 0 and h == 1:
+                        turn_next(1)
+                    if i == 1:
+                        turn_next(2 * h)
+                        if STEADY_S and h % STEADY_S == STEADY_S - 1:
+                            turn_next(2 * h)
+                    if i == TK:
+                        turn_keys(c // 2, c % 2)
+                if i == (KSLOT if has_k else 0) and c - 1 < halves:
                     copy_keys((c - 1) // 2, (c - 1) % 2)
-                if i == 1 and owed:
-                    copy_y(*owed[0], False)
-                    owed = owed[1:]
-                if i == 2:
-                    if has_k:
-                        copy_y(yg, y0 // 2, True)
+                if has_k:
+                    if i == 0 and STEADY_S and h % STEADY_S == 0 and h > 1:
+                        copy_next(False)
+                    if i == 2:
+                        copy_next(True)
                         scale_y(yg, c0 + pool, c0 + unit, nc.vector)
                         store_y(yg, y0, y0 + 4)
-                    if widened < min(c + 2, halves):
-                        widen(widened // 2, widened % 2)
-                        widened = widened + 1
+                    if c + 1 < halves and i < 3 and i != KSLOT:
+                        part = 1 if i == 2 else 0
+                        widen((c + 1) // 2, (c + 1) % 2, bool(part and CAST_V and h % CAST_V == 0), (part,))
+                    if i == 3 and c + 1 == halves:
+                        turn_next(2 * h)
+                        turn_next(2 * h)
+                else:
+                    if i < LS:
+                        copy_next(False)
+                    turn_next(2 * h)
+                    turn_next(2 * h)
+                if i == 2:
                     if h % 2 == 0 and g + 1 < GROUPS:
                         quantise_keys(g + 1)
-                    if h % 2 == 1 and g > 0:
-                        quantise_y(g - 1)
-                    if on_v and not has_k:
-                        copy_y(yg, y0 // 2, True)
-            owed = owed + ([] if on_v else [(yg, y0 // 2)]) + [(yg, y0 // 2 + 1)]
+                    if 4 * state["quantised"] + 4 <= done or not has_k:
+                        quantise_next()
         g = GROUPS - 1
         round_y(g, 4, 6)
-        for pair in owed:
-            copy_y(*pair, False)
-        turn_y(g, 2)
-        round_y(g, 6, 7)
-        turn_one(g, 6)
-        round_y(g, 7, 8)
-        turn_one(g, 7)
-        scale_y(g, 4 * GROUP, (8 - TAIL_S) * GROUP, nc.vector)
-        store_y(g, 4, 8 - TAIL_S)
-        copy_y(g, 2, False)
-        copy_one(g, 6, False)
-        copy_one(g, 7, False)
-        if TAIL_S:
-            scale_y(g, (8 - TAIL_S) * GROUP, 8 * GROUP, nc.scalar)
-            store_y(g, 8 - TAIL_S, 8)
-        quantise_y(g)
+        round_y(g, 6, 8)
+        if TAIL_S < 4:
+            scale_y(g, 4 * GROUP, (8 - TAIL_S) * GROUP, nc.vector)
+            store_y(g, 4, 8 - TAIL_S)
+        n = 0
+        while state["copied"] < 4 * GROUPS:
+            copy_next(state["copied"] in TAIL_V)
+            turn_next(4 * GROUPS)
+            turn_next(4 * GROUPS)
+            if n == TAIL_AT and TAIL_S:
+                scale_y(g, (8 - TAIL_S) * GROUP, 8 * GROUP, nc.scalar)
+                store_y(g, 8 - TAIL_S, 8)
+            quantise_next()
+            n = n + 1

@@ -17,29 +17,27 @@ ALU = mybir.AluOpType
 ACT = mybir.ActivationFunctionType
 
 P = 128
-GROUP = 512
+PACK = 4
+GROUP = P * PACK
 GROUPS = S // GROUP
+PARTS = 2 * GROUPS
 TILES = H * T // P
-POOL_COLS = 1536
-H1_POOL = 0
-HEAD_V = 0
-WARM_N = 256
-WARM_FROM = 1
-WARM_TO = 64
-LS = 1
-LV = 1
-LATE_POOL = 512
-STEADY_S = 0
-AHEAD = 3
-TAIL_S = 0
-KSLOT = 1
-BATCHES = [(0, 3), (3, 8)]
-CAST_V = 0
-TAIL_V = (30,)
-TAIL_AT = 0
-TK = 2
-ACT_FIRST = True
-MEAN_PSUM = True
+STEP_TILES = 4
+STEP_COLS = STEP_TILES * GROUP
+STEPS = GROUPS * TILES // STEP_TILES
+ROW_WORDS = D // 2
+PAIRS = TILES // 2
+BLOCKS = D // B
+
+RAW_BANKS = 3
+TURN_BANKS = 4
+TURNED_AHEAD = 2
+PART_LEAD = 4
+
+POOL_COLS_LONG = 1280
+POOL_COLS_SHORT = 896
+
+SCALE_BATCHES = ((0, 3), (3, GROUPS))
 
 
 def tile_centred_key_capped_logits_b15_kernel(
@@ -55,32 +53,27 @@ def tile_centred_key_capped_logits_b15_kernel(
         psum = ctx.enter_context(tc.psum_pool(name="psum", bufs=1))
         ctx.enter_context(tc.manual_schedule())
 
-        key_bytes = {}
+        key_bytes, q_words = {}, {}
 
         def load_keys(g):
-            tile = keep.tile([P, 4 * D], U8, name="key_bytes", bufs=GROUPS, align_bytes=64)
-            nc.sync.dma_start(out=tile[:], in_=keys_bytes[g * GROUP:(g + 1) * GROUP, :].rearrange("(p j) d -> p (j d)", j=4))
-            key_bytes[g] = tile
-
-        load_keys(0)
-        key_scale = keep.tile([P, GROUPS, 16], F32, name="key_scale")
-        nc.sync.dma_start(out=key_scale[:], in_=keys_scale.rearrange("(g p j) b -> p g (j b)", p=P, j=4))
-        if MEAN_PSUM:
-            mean_words = keep.tile([P, 2], F32, name="mean_words")
-            with nc.allow_non_contiguous_dma(reason="one word of the mean to a partition"):
-                nc.sync.dma_start(out=mean_words[:], in_=keys_mean.bitcast(F32).rearrange("o (h p) -> p (o h)", p=P))
-        else:
-            mean_sb = keep.tile([P, D], BF16, name="mean_sb")
-            nc.sync.dma_start(out=mean_sb[:], in_=keys_mean.rearrange("o d -> (o d)").partition_broadcast(P))
-        q_raw = {}
+            key_bytes[g] = keep.tile([P, PACK * D], U8, name="key_bytes", bufs=GROUPS, align_bytes=64)
+            rows = keys_bytes[g * GROUP:(g + 1) * GROUP, :]
+            nc.sync.dma_start(out=key_bytes[g][:], in_=rows.rearrange("(p j) d -> p (j d)", j=PACK))
 
         def load_queries(first, last):
             tile = keep.tile([P, 2 * (last - first), D], BF16, name="q_raw", bufs=3)
             nc.sync.dma_start(out=tile[:], in_=q_rows[:, 2 * first:2 * last, :])
             words = tile[:].rearrange("p m d -> p (m d)").bitcast(F32)
             for pair in range(first, last):
-                q_raw[pair] = words[:, (pair - first) * 512:(pair - first + 1) * 512]
+                at = (pair - first) * 2 * ROW_WORDS
+                q_words[pair] = words[:, at:at + 2 * ROW_WORDS]
 
+        load_keys(0)
+        key_scale = keep.tile([P, GROUPS, PACK * BLOCKS], F32, name="key_scale")
+        nc.sync.dma_start(out=key_scale[:], in_=keys_scale.rearrange("(g p j) b -> p g (j b)", p=P, j=PACK))
+        mean_words = keep.tile([P, 2], F32, name="mean_words")
+        with nc.allow_non_contiguous_dma(reason="words p and 128 + p of the mean go to partition p"):
+            nc.sync.dma_start(out=mean_words[:], in_=keys_mean.bitcast(F32).rearrange("o (w p) -> p (o w)", p=P))
         load_queries(0, 1)
         load_keys(1)
         cap_all = keep.tile([P, H], BF16, name="cap_all")
@@ -88,29 +81,28 @@ def tile_centred_key_capped_logits_b15_kernel(
         temp_sb = keep.tile([P, TILES], BF16, name="temp_sb")
         nc.sync.dma_start(out=temp_sb[:], in_=temp.rearrange("h (a m) o -> (h a) (m o)", m=TILES))
         load_queries(1, 2)
-        load_queries(2, 4)
+        load_queries(2, PAIRS)
         for g in range(2, GROUPS):
             load_keys(g)
 
         ident = keep.tile([P, P], F32, name="ident")
         make_identity(nc, ident[:])
+        span = P // H
         head_mask = keep.tile([P, H], F32, name="head_mask")
         nc.gpsimd.memset(head_mask[:], 1.0)
-        nc.gpsimd.affine_select(out=head_mask[:], in_=head_mask[:], pattern=[[-8, H]], compare_op=ALU.is_ge,
+        nc.gpsimd.affine_select(out=head_mask[:], in_=head_mask[:], pattern=[[-span, H]], compare_op=ALU.is_ge,
                                 fill=0.0, base=0, channel_multiplier=1)
-        nc.gpsimd.affine_select(out=head_mask[:], in_=head_mask[:], pattern=[[8, H]], compare_op=ALU.is_ge,
-                                fill=0.0, base=7, channel_multiplier=-1)
+        nc.gpsimd.affine_select(out=head_mask[:], in_=head_mask[:], pattern=[[span, H]], compare_op=ALU.is_ge,
+                                fill=0.0, base=span - 1, channel_multiplier=-1)
+        mean_bank = psum.tile([P, 2, P], F32, name="mean_bank")
+        for w in range(2):
+            nc.tensor.transpose(mean_bank[:, w, :], mean_words[:, w:w + 1].to_broadcast([P, P]), ident[:])
+        mean_row = mean_bank[:].rearrange("p w c -> p (w c)").bitcast(BF16)
 
-        if MEAN_PSUM:
-            mean_bank = psum.tile([P, 2, P], F32, name="mean_bank")
-            for h in range(2):
-                nc.tensor.transpose(mean_bank[:, h, :], mean_words[:, h:h + 1].to_broadcast([P, P]), ident[:])
-            mean_row = mean_bank[:].rearrange("p h w -> p (h w)").bitcast(BF16)
-        else:
-            mean_row = mean_sb[:]
-
-        def turn_bank():
-            return psum.tile([P, 4, P], F32, name="turn", bufs=4)
+        picked = keep.tile([P, H], F32, name="picked")
+        cap_col = keep.tile([P, 1], F32, name="cap_col")
+        inv_cap = keep.tile([P, 1], F32, name="inv_cap")
+        slope = keep.tile([P, TILES], F32, name="slope")
 
         def copy_on(vector, out, in_):
             if vector:
@@ -118,285 +110,247 @@ def tile_centred_key_capped_logits_b15_kernel(
             else:
                 nc.scalar.copy(out=out, in_=in_)
 
-        wide, value, kbank, kgroup, kq = {}, {}, {}, {}, {}
-
-        def widen(g, half, vector=False, parts=(0, 1)):
-            if parts[0] == 0:
-                wide[g, half] = work.tile([P, 2 * D], BF16, name="wide", bufs=5)
-            lo, hi = parts[0] * D, (parts[-1] + 1) * D
-            codes = key_bytes[g][:, half * 2 * D + lo:half * 2 * D + hi].bitcast(FP8)
-            if ACT_FIRST and (g, half) == (0, 1):
-                nc.scalar.activation(out=wide[g, half][:, lo:hi], in_=codes, func=ACT.Copy)
-            else:
-                copy_on(vector, wide[g, half][:, lo:hi], codes)
-
-        def dequantise(g, half):
-            tile = work.tile([P, 2 * D], BF16, name="value", bufs=4)
-            for jj in range(2):
-                for b in range(4):
-                    cols = slice(jj * D + b * B, jj * D + (b + 1) * B)
-                    col = 4 * (2 * half + jj) + b
-                    nc.vector.scalar_tensor_tensor(
-                        out=tile[:, cols], in0=wide[g, half][:, cols], scalar=key_scale[:, g, col:col + 1],
-                        in1=mean_row[:, b * B:(b + 1) * B], op0=ALU.mult, op1=ALU.add)
-            value[g, half] = tile
-
         def turn_rows(words):
-            bank = turn_bank()
+            bank = psum.tile([P, 4, P], F32, name="turn", bufs=TURN_BANKS)
             for r in range(2):
                 for u in range(2):
-                    nc.tensor.transpose(bank[:, 2 * r + u, :], words[:, r * 256 + u:(r + 1) * 256:2], ident[:])
+                    every_second = words[:, r * ROW_WORDS + u:(r + 1) * ROW_WORDS:2]
+                    nc.tensor.transpose(bank[:, 2 * r + u, :], every_second, ident[:])
             return bank
 
-        def turn_keys(g, half):
-            kbank[g, half] = turn_rows(value[g, half][:].bitcast(F32))
+        wide, value, key_bank, key_grouped, key_mx = {}, {}, {}, {}, {}
 
-        def copy_keys(g, half, vector=False):
+        def part_bytes(part):
+            wide[part] = work.tile([P, 2 * D], BF16, name="wide", bufs=5)
+            at = (part % 2) * 2 * D
+            return key_bytes[part // 2][:, at:at + 2 * D].bitcast(FP8)
+
+        def widen(part, vector=False):
+            stored = part_bytes(part)
+            copy_on(vector, wide[part][:], stored)
+
+        def dequantise(part):
+            value[part] = work.tile([P, 2 * D], BF16, name="value", bufs=4)
+            for r in range(2):
+                for b in range(BLOCKS):
+                    cols = slice(r * D + b * B, r * D + (b + 1) * B)
+                    at = BLOCKS * (2 * (part % 2) + r) + b
+                    nc.vector.scalar_tensor_tensor(
+                        out=value[part][:, cols], in0=wide[part][:, cols], scalar=key_scale[:, part // 2, at:at + 1],
+                        in1=mean_row[:, b * B:(b + 1) * B], op0=ALU.mult, op1=ALU.add)
+
+        def turn_keys(part):
+            key_bank[part] = turn_rows(value[part][:].bitcast(F32))
+
+        def copy_keys(part):
+            g, half = divmod(part, 2)
             if half == 0:
-                kgroup[g] = work.tile([P, GROUP * 4], BF16, name="kgroup", bufs=2, align_bytes=64)
-            out = kgroup[g][:].bitcast(F32).rearrange("c (p w) -> c p w", w=8)[:, :, 4 * half:4 * half + 4]
-            copy_on(vector, out, kbank[g, half][:].rearrange("c w p -> c p w"))
+                key_grouped[g] = work.tile([P, GROUP * PACK], BF16, name="key_grouped", align_bytes=64)
+            words = key_grouped[g][:].bitcast(F32).rearrange("c (p w) -> c p w", w=2 * PACK)
+            nc.scalar.copy(out=words[:, :, 4 * half:4 * half + 4], in_=key_bank[part][:].rearrange("c w p -> c p w"))
 
         def quantise_keys(g):
-            codes = work.tile([P, GROUP], U32, name="kcodes", bufs=3, align_bytes=64)
-            scales = work.tile([P, GROUP], U8, name="kscales", bufs=3, align_bytes=64)
-            nc.vector.quantize_mx(out=codes[:].bitcast(FP8X4), scales=scales[:], in_=kgroup[g][:])
-            kq[g] = (codes, scales)
+            codes = work.tile([P, GROUP], U32, name="key_codes", bufs=3, align_bytes=64)
+            scales = work.tile([P, GROUP], U8, name="key_scales", bufs=3, align_bytes=64)
+            nc.vector.quantize_mx(out=codes[:].bitcast(FP8X4), scales=scales[:], in_=key_grouped[g][:])
+            key_mx[g] = (codes, scales)
 
-        qbank, qgroup, qq = {}, {}, {}
+        q_bank, q_grouped, q_mx = {}, {}, {}
 
         def turn_queries(pair):
-            qbank[pair] = turn_rows(q_raw[pair])
+            q_bank[pair] = turn_rows(q_words[pair])
 
         def copy_queries(pair, vector=False):
-            qgroup[pair] = keep.tile([P, 2 * P * 4], BF16, name="qgroup", bufs=4, align_bytes=64)
-            copy_on(vector, qgroup[pair][:].bitcast(F32).rearrange("c (r p u) -> c r p u", r=2, u=2),
-                    qbank[pair][:].rearrange("c (r u) p -> c r p u", u=2))
+            q_grouped[pair] = keep.tile([P, 2 * P * PACK], BF16, name="q_grouped", bufs=PAIRS, align_bytes=64)
+            copy_on(vector, q_grouped[pair][:].bitcast(F32).rearrange("c (r p u) -> c r p u", r=2, u=2),
+                    q_bank[pair][:].rearrange("c (r u) p -> c r p u", u=2))
 
         def quantise_queries(pair):
-            codes = keep.tile([P, 2 * P], U32, name="qcodes", bufs=4, align_bytes=64)
-            scales = keep.tile([P, 2 * P], U8, name="qscales", bufs=4, align_bytes=64)
-            nc.vector.quantize_mx(out=codes[:].bitcast(FP8X4), scales=scales[:], in_=qgroup[pair][:])
-            qq[pair] = (codes, scales)
+            codes = keep.tile([P, 2 * P], U32, name="q_codes", bufs=PAIRS, align_bytes=64)
+            scales = keep.tile([P, 2 * P], U8, name="q_scales", bufs=PAIRS, align_bytes=64)
+            nc.vector.quantize_mx(out=codes[:].bitcast(FP8X4), scales=scales[:], in_=q_grouped[pair][:])
+            q_mx[pair] = (codes, scales)
 
-        picked = keep.tile([P, H], F32, name="picked")
-        cap_col = keep.tile([P, 1], F32, name="cap_col")
-        inv_cap = keep.tile([P, 1], F32, name="inv_cap")
-        slope = keep.tile([P, TILES], F32, name="slope")
-        consts = {"cap": cap_col, "slope": slope}
+        raw, logits = {}, {}
 
-        raw, ty = {}, {}
-
-        def multiply(g, m):
-            bank = psum.tile([P, GROUP], F32, name="raw", bufs=3)
+        def multiply(n):
+            g, m = divmod(n, TILES)
+            raw[n] = psum.tile([P, GROUP], F32, name="raw", bufs=RAW_BANKS)
             cols = slice((m % 2) * P, (m % 2 + 1) * P)
-            if WARM_N and WARM_FROM <= TILES * g + m < WARM_TO:
-                nc.tensor.matmul_mx(out=bank[:, 0:WARM_N], lhsT=qq[m // 2][0][:, cols].bitcast(FP8X4), lhsT_scale=qq[m // 2][1][:, cols],
-                                    rhs=kq[g][0][:, 0:WARM_N].bitcast(FP8X4), rhs_scale=kq[g][1][:, 0:WARM_N], start=True, stop=True)
-            nc.tensor.matmul_mx(out=bank[:], lhsT=qq[m // 2][0][:, cols].bitcast(FP8X4), lhsT_scale=qq[m // 2][1][:, cols],
-                                rhs=kq[g][0][:].bitcast(FP8X4), rhs_scale=kq[g][1][:], start=True, stop=True)
-            raw[g, m] = bank
+            nc.tensor.matmul_mx(
+                out=raw[n][:], lhsT=q_mx[m // 2][0][:, cols].bitcast(FP8X4), lhsT_scale=q_mx[m // 2][1][:, cols],
+                rhs=key_mx[g][0][:].bitcast(FP8X4), rhs_scale=key_mx[g][1][:], start=True, stop=True)
 
-        def squash(g, m):
+        def squash(n):
+            g, m = divmod(n, TILES)
             if m == 0:
-                ty[g] = work.tile([P, TILES, GROUP], F32, name="ty", bufs=4)
-            nc.scalar.activation(out=ty[g][:, m, :], in_=raw[g, m][:], func=ACT.Tanh, scale=consts["slope"][:, m:m + 1])
+                logits[g] = work.tile([P, TILES, GROUP], F32, name="logits", bufs=4)
+            nc.scalar.activation(out=logits[g][:, m, :], in_=raw[n][:], func=ACT.Tanh, scale=slope[:, m:m + 1])
 
-        rounded, ybank, ygroup, yscales = {}, {}, {}, {}
+        def step_tiles(step, first, last):
+            g, m = divmod(step * STEP_TILES, TILES)
+            return g, slice(m + first, m + last)
 
-        def round_y(g, m0, m1):
-            if m0 % 4 == 0:
-                rounded[g, m0 // 4] = work.tile([P, 2, 4, 256], BF16, name="rounded", bufs=8)
+        rounded = {}
+
+        def round_y(step, first, last):
+            g, tiles = step_tiles(step, first, last)
+            if first == 0:
+                rounded[step] = work.tile([P, 2, STEP_TILES, GROUP // 2], BF16, name="rounded", bufs=8)
             nc.vector.tensor_scalar(
-                out=rounded[g, m0 // 4][:, :, m0 % 4:m0 % 4 + m1 - m0, :].rearrange("q u m (p e) -> q u (m p) e", e=2),
-                in0=ty[g][:, m0:m1, :].rearrange("q m (p u e) -> q u (m p) e", u=2, e=2),
-                scalar1=consts["cap"][:], scalar2=None, op0=ALU.mult)
+                out=rounded[step][:, :, first:last, :].rearrange("q u m (p e) -> q u (m p) e", e=2),
+                in0=logits[g][:, tiles, :].rearrange("q m (p u e) -> q u (m p) e", u=2, e=2),
+                scalar1=cap_col[:], scalar2=None, op0=ALU.mult)
 
-        def scale_y(g, c0, c1, engine):
-            view = ty[g][:].rearrange("q m s -> q (m s)")[:, c0:c1]
-            if engine is nc.scalar:
-                engine.activation(out=view, in_=view, func=ACT.Copy, scale=consts["cap"][:])
-            elif engine is nc.gpsimd:
-                engine.tensor_scalar(out=view, in0=view, scalar1=consts["cap"][:], scalar2=1.0, op0=ALU.mult, op1=ALU.mult)
-            else:
-                engine.tensor_scalar(out=view, in0=view, scalar1=consts["cap"][:], scalar2=None, op0=ALU.mult)
+        def step_columns(step, first, last):
+            g, tiles = step_tiles(step, 0, STEP_TILES)
+            return logits[g][:, tiles, :].rearrange("q m s -> q (m s)")[:, first:last]
 
-        def store_y(g, m0, m1):
-            nc.sync.dma_start(out=y_rows[:, m0:m1, g * GROUP:(g + 1) * GROUP], in_=ty[g][:, m0:m1, :])
+        def scale_on_gpsimd(step, cols):
+            view = step_columns(step, 0, cols)
+            nc.gpsimd.tensor_scalar(out=view, in0=view, scalar1=cap_col[:], scalar2=1.0, op0=ALU.mult, op1=ALU.mult)
 
-        def turn_y(g, pair):
-            bank = turn_bank()
-            for r in range(2):
-                tile, at = rounded[g, pair // 2], 2 * (pair % 2) + r
-                for u in range(2):
-                    nc.tensor.transpose(bank[:, 2 * r + u, :], tile[:, u, at, :].bitcast(F32), ident[:])
-            ybank[g, pair] = bank
+        def scale_rest_and_store(step, done):
+            view = step_columns(step, done, STEP_COLS)
+            nc.vector.tensor_scalar(out=view, in0=view, scalar1=cap_col[:], scalar2=None, op0=ALU.mult)
+            g, tiles = step_tiles(step, 0, STEP_TILES)
+            nc.sync.dma_start(out=y_rows[:, tiles, g * GROUP:(g + 1) * GROUP], in_=logits[g][:, tiles, :])
 
-        def copy_y(g, pair, vector):
-            if g not in ygroup:
-                ygroup[g] = work.tile([P, H * T * 4], BF16, name="ygroup", bufs=3, align_bytes=64)
-            out = ygroup[g][:].bitcast(F32).rearrange("p (q w) -> p q w", w=2 * TILES)[:, :, 4 * pair:4 * pair + 4]
-            copy_on(vector, out, ybank[g, pair][:].rearrange("p w q -> p q w"))
+        y_bank, y_grouped, y_scales = {}, {}, {}
+        queue = {"turned": 0, "copied": 0, "quantised": 0}
 
-        batches = BATCHES
+        def turn_next(steps_rounded):
+            n = queue["turned"]
+            if n < 2 * steps_rounded and n - queue["copied"] < TURNED_AHEAD:
+                y_bank[n] = psum.tile([P, 4, P], F32, name="turn", bufs=TURN_BANKS)
+                for r in range(2):
+                    for u in range(2):
+                        words = rounded[n // 2][:, u, 2 * (n % 2) + r, :].bitcast(F32)
+                        nc.tensor.transpose(y_bank[n][:, 2 * r + u, :], words, ident[:])
+                queue["turned"] = n + 1
 
-        def quantise_y(g):
-            first, last = [b for b in batches if b[0] <= g < b[1]][0]
-            if g == first:
-                yscales[first] = keep.tile([P, last - first, H * T], U8, name="yscales", bufs=len(BATCHES), align_bytes=64)
-            codes = work.tile([P, H * T], U32, name="ycodes", bufs=5, align_bytes=64)
-            nc.vector.quantize_mx(out=codes[:].bitcast(FP8X4), scales=yscales[first][:, g - first, :], in_=ygroup[g][:])
-            nc.sync.dma_start(out=out_1[g].rearrange("p m t -> p (m t)").bitcast(I32), in_=codes[:].bitcast(I32))
-            if g == last - 1:
-                for quad in range(4):
-                    nc.sync.dma_start(
-                        out=out_2[first:last, 4 * quad:4 * quad + 4, :].rearrange("g r m -> r g m").bitcast(I32),
-                        in_=yscales[first][32 * quad:32 * quad + 4, :, :].bitcast(I32))
+        def copy_next(vector):
+            n = queue["copied"]
+            if n < queue["turned"]:
+                g, pair = divmod(n, PAIRS)
+                if pair == 0:
+                    y_grouped[g] = work.tile([P, H * T * PACK], BF16, name="y_grouped", bufs=3, align_bytes=64)
+                words = y_grouped[g][:].bitcast(F32).rearrange("p (q w) -> p q w", w=2 * TILES)
+                copy_on(vector, words[:, :, 4 * pair:4 * pair + 4], y_bank[n][:].rearrange("p w q -> p q w"))
+                queue["copied"] = n + 1
 
-        widen(0, 0, True)
-        widen(0, 1)
-        dequantise(0, 0)
+        def quantise_next():
+            g = queue["quantised"]
+            if PAIRS * (g + 1) <= queue["copied"]:
+                first, last = [batch for batch in SCALE_BATCHES if batch[0] <= g < batch[1]][0]
+                if g == first:
+                    y_scales[first] = keep.tile([P, last - first, H * T], U8, name="y_scales",
+                                                bufs=len(SCALE_BATCHES), align_bytes=64)
+                codes = work.tile([P, H * T], U32, name="y_codes", bufs=5, align_bytes=64)
+                nc.vector.quantize_mx(out=codes[:].bitcast(FP8X4), scales=y_scales[first][:, g - first, :],
+                                      in_=y_grouped[g][:])
+                nc.sync.dma_start(out=out_1[g].rearrange("p m t -> p (m t)").bitcast(I32), in_=codes[:].bitcast(I32))
+                if g == last - 1:
+                    for quad in range(4):
+                        rows = out_2[first:last, 4 * quad:4 * quad + 4, :].rearrange("g r m -> r g m")
+                        nc.sync.dma_start(out=rows.bitcast(I32),
+                                          in_=y_scales[first][32 * quad:32 * quad + 4, :, :].bitcast(I32))
+                queue["quantised"] = g + 1
+
+        widen(0, vector=True)
+        stored = part_bytes(1)
+        nc.scalar.activation(out=wide[1][:], in_=stored, func=ACT.Copy)
+        dequantise(0)
         nc.vector.tensor_tensor(out=picked[:], in0=cap_all[:], in1=head_mask[:], op=ALU.mult)
-        dequantise(0, 1)
+        dequantise(1)
         nc.vector.tensor_reduce(out=cap_col[:], in_=picked[:], op=ALU.add, axis=mybir.AxisListType.X)
         turn_queries(0)
-        turn_keys(0, 0)
-        turn_keys(0, 1)
+        turn_keys(0)
+        turn_keys(1)
         turn_queries(1)
-        widen(1, 0)
+        widen(2)
         copy_queries(0)
-        widen(1, 1)
-        copy_keys(0, 0)
-        copy_keys(0, 1)
+        widen(3)
+        copy_keys(0)
+        copy_keys(1)
         quantise_queries(0)
         nc.vector.reciprocal(out=inv_cap[:], in_=cap_col[:])
-        dequantise(1, 0)
+        dequantise(2)
         nc.vector.tensor_scalar(out=slope[:], in0=temp_sb[:], scalar1=inv_cap[:], scalar2=None, op0=ALU.mult)
         quantise_keys(0)
         copy_queries(1)
-        widen(2, 0)
+        widen(4)
         turn_queries(2)
-        multiply(0, 0)
-        multiply(0, 1)
+        multiply(0)
+        multiply(1)
         quantise_queries(1)
-        multiply(0, 2)
-        dequantise(1, 1)
+        multiply(2)
+        dequantise(3)
         copy_queries(2)
-        squash(0, 0)
+        squash(0)
         turn_queries(3)
-        multiply(0, 3)
-        squash(0, 1)
-        dequantise(2, 0)
+        multiply(3)
+        squash(1)
+        dequantise(4)
         quantise_queries(2)
-        turn_keys(1, 0)
-        multiply(0, 4)
-        copy_queries(3, True)
-        widen(2, 1, True)
-        squash(0, 2)
-        turn_keys(1, 1)
-        multiply(0, 5)
+        turn_keys(2)
+        multiply(4)
+        copy_queries(3, vector=True)
+        widen(5, vector=True)
+        squash(2)
+        turn_keys(3)
+        multiply(5)
         quantise_queries(3)
-        squash(0, 3)
-        copy_keys(1, 0, HEAD_V > 0)
-        multiply(0, 6)
-        turn_keys(2, 0)
-        copy_keys(1, 1, HEAD_V > 1)
-        halves = 2 * GROUPS
-        unit = 4 * GROUP
-        state = {"turned": 0, "copied": 0, "quantised": 0}
+        squash(3)
+        copy_keys(2)
+        multiply(6)
+        turn_keys(4)
+        copy_keys(3)
 
-        def turn_next(limit):
-            n = state["turned"]
-            if n < limit and n - state["copied"] < AHEAD:
-                turn_y(n // 4, n % 4)
-                state["turned"] = n + 1
-
-        def copy_next(vector):
-            n = state["copied"]
-            if n < state["turned"]:
-                copy_y(n // 4, n % 4, vector)
-                state["copied"] = n + 1
-
-        def quantise_next():
-            g = state["quantised"]
-            if 4 * g + 4 <= state["copied"]:
-                quantise_y(g)
-                state["quantised"] = g + 1
-
-        for h in range(1, halves):
-            g, m0 = h // 2, 4 * (h % 2)
-            c = h + 4
-            has_k = c < halves
-            yg, y0 = (h - 1) // 2, 4 * ((h - 1) % 2)
-            c0 = y0 * GROUP
-            pool = (POOL_COLS if h > 1 else H1_POOL) if has_k else LATE_POOL
-            first = (pool + GROUP - 1) // GROUP if pool else 2
-            ahead = [((h + (i + 3) // 4) // 2, (m0 + i + 3) % TILES) for i in range(4)]
-            done = state["copied"]
-            round_y(yg, y0, y0 + first)
-            if pool:
-                scale_y(yg, c0, c0 + pool, nc.gpsimd)
-            round_y(yg, y0 + first, y0 + 4)
-            if h == 1:
+        for step in range(1, STEPS):
+            part = step + PART_LEAD
+            keys_left = part < PARTS
+            odd = step % 2 == 1
+            pool_cols = (POOL_COLS_LONG if odd else POOL_COLS_SHORT) if keys_left and step > 1 else 0
+            split = -(-pool_cols // GROUP) if pool_cols else STEP_TILES // 2
+            round_y(step - 1, 0, split)
+            if pool_cols:
+                scale_on_gpsimd(step - 1, pool_cols)
+            round_y(step - 1, split, STEP_TILES)
+            if step == 1:
                 quantise_keys(1)
-            if has_k:
-                dequantise(c // 2, c % 2)
-            else:
-                for j in range(LV):
-                    copy_next(True)
-                scale_y(yg, c0 + pool, c0 + unit, nc.vector)
-                store_y(yg, y0, y0 + 4)
-            for i in range(4):
-                squash(g, m0 + i)
-                if ahead[i][0] < GROUPS:
-                    multiply(*ahead[i])
-                if has_k:
-                    if i == 0 and h == 1:
-                        turn_next(1)
-                    if i == 1:
-                        turn_next(2 * h)
-                        if STEADY_S and h % STEADY_S == STEADY_S - 1:
-                            turn_next(2 * h)
-                    if i == TK:
-                        turn_keys(c // 2, c % 2)
-                if i == (KSLOT if has_k else 0) and c - 1 < halves:
-                    copy_keys((c - 1) // 2, (c - 1) % 2)
-                if has_k:
-                    if i == 0 and STEADY_S and h % STEADY_S == 0 and h > 1:
-                        copy_next(False)
-                    if i == 2:
-                        copy_next(True)
-                        scale_y(yg, c0 + pool, c0 + unit, nc.vector)
-                        store_y(yg, y0, y0 + 4)
-                    if c + 1 < halves and i < 3 and i != KSLOT:
-                        part = 1 if i == 2 else 0
-                        widen((c + 1) // 2, (c + 1) % 2, bool(part and CAST_V and h % CAST_V == 0), (part,))
-                    if i == 3 and c + 1 == halves:
-                        turn_next(2 * h)
-                        turn_next(2 * h)
+            if keys_left:
+                dequantise(part)
+            for i in range(STEP_TILES):
+                n = step * STEP_TILES + i
+                squash(n)
+                if n + RAW_BANKS < GROUPS * TILES:
+                    multiply(n + RAW_BANKS)
+                if i == 0:
+                    copy_next(vector=False)
+                if i == 1:
+                    if part - 1 < PARTS:
+                        copy_keys(part - 1)
+                    if keys_left and odd:
+                        copy_next(vector=True)
+                    scale_rest_and_store(step - 1, pool_cols)
+                if i == 2 and part + 1 < PARTS:
+                    widen(part + 1)
+                if i == 2 and keys_left:
+                    turn_keys(part)
                 else:
-                    if i < LS:
-                        copy_next(False)
-                    turn_next(2 * h)
-                    turn_next(2 * h)
+                    turn_next(step)
                 if i == 2:
-                    if h % 2 == 0 and g + 1 < GROUPS:
-                        quantise_keys(g + 1)
-                    if 4 * state["quantised"] + 4 <= done or not has_k:
+                    if not odd and part - 1 < PARTS:
+                        quantise_keys((part - 1) // 2)
+                    if odd or not keys_left:
                         quantise_next()
-        g = GROUPS - 1
-        round_y(g, 4, 6)
-        round_y(g, 6, 8)
-        if TAIL_S < 4:
-            scale_y(g, 4 * GROUP, (8 - TAIL_S) * GROUP, nc.vector)
-            store_y(g, 4, 8 - TAIL_S)
-        n = 0
-        while state["copied"] < 4 * GROUPS:
-            copy_next(state["copied"] in TAIL_V)
-            turn_next(4 * GROUPS)
-            turn_next(4 * GROUPS)
-            if n == TAIL_AT and TAIL_S:
-                scale_y(g, (8 - TAIL_S) * GROUP, 8 * GROUP, nc.scalar)
-                store_y(g, 8 - TAIL_S, 8)
+
+        round_y(STEPS - 1, 0, STEP_TILES // 2)
+        round_y(STEPS - 1, STEP_TILES // 2, STEP_TILES)
+        scale_rest_and_store(STEPS - 1, 0)
+        while queue["copied"] < PAIRS * GROUPS:
+            copy_next(vector=False)
+            turn_next(STEPS)
+            turn_next(STEPS)
             quantise_next()
-            n = n + 1

from contextlib import ExitStack

import concourse.mybir as mybir
from concourse.masks import make_identity

S, D, H, T, B = 4096, 512, 16, 64, 128
FLOPS = 2 * H * T * S * D

F32 = mybir.dt.float32
BF16 = mybir.dt.bfloat16
I32 = mybir.dt.int32
U32 = mybir.dt.uint32
U8 = mybir.dt.uint8
FP8 = mybir.dt.float8_e4m3fn
FP8X4 = mybir.dt.float8_e4m3fn_x4
ALU = mybir.AluOpType
ACT = mybir.ActivationFunctionType

P = 128
PACK = 4
GROUP = P * PACK
GROUPS = S // GROUP
PARTS = 2 * GROUPS
TILES = H * T // P
STEP_TILES = 4
STEP_COLS = STEP_TILES * GROUP
STEPS = GROUPS * TILES // STEP_TILES
ROW_WORDS = D // 2
PAIRS = TILES // 2
BLOCKS = D // B

RAW_BANKS = 3
TURN_BANKS = 4
TURNED_AHEAD = 2
PART_LEAD = 4

POOL_COLS_LONG = 1280
POOL_COLS_SHORT = 896

SCALE_BATCHES = ((0, 3), (3, GROUPS))


def tile_centred_key_capped_logits_b15_kernel(
    tc, keys_bytes, keys_scale, keys_mean, queries, temp, cap, out_0, out_1, out_2
):
    nc = tc.nc
    y_rows = out_0.rearrange("h (a m) s -> (h a) m s", m=TILES)
    q_rows = queries.rearrange("h (a m) d -> (h a) m d", m=TILES)

    with ExitStack() as ctx:
        keep = ctx.enter_context(tc.tile_pool(name="keep", bufs=1))
        work = ctx.enter_context(tc.tile_pool(name="work", bufs=2))
        psum = ctx.enter_context(tc.psum_pool(name="psum", bufs=1))
        ctx.enter_context(tc.manual_schedule())

        key_bytes, q_words = {}, {}

        def load_keys(g):
            key_bytes[g] = keep.tile([P, PACK * D], U8, name="key_bytes", bufs=GROUPS, align_bytes=64)
            rows = keys_bytes[g * GROUP:(g + 1) * GROUP, :]
            nc.sync.dma_start(out=key_bytes[g][:], in_=rows.rearrange("(p j) d -> p (j d)", j=PACK))

        def load_queries(first, last):
            tile = keep.tile([P, 2 * (last - first), D], BF16, name="q_raw", bufs=3)
            nc.sync.dma_start(out=tile[:], in_=q_rows[:, 2 * first:2 * last, :])
            words = tile[:].rearrange("p m d -> p (m d)").bitcast(F32)
            for pair in range(first, last):
                at = (pair - first) * 2 * ROW_WORDS
                q_words[pair] = words[:, at:at + 2 * ROW_WORDS]

        load_keys(0)
        key_scale = keep.tile([P, GROUPS, PACK * BLOCKS], F32, name="key_scale")
        nc.sync.dma_start(out=key_scale[:], in_=keys_scale.rearrange("(g p j) b -> p g (j b)", p=P, j=PACK))
        mean_words = keep.tile([P, 2], F32, name="mean_words")
        with nc.allow_non_contiguous_dma(reason="words p and 128 + p of the mean go to partition p"):
            nc.sync.dma_start(out=mean_words[:], in_=keys_mean.bitcast(F32).rearrange("o (w p) -> p (o w)", p=P))
        load_queries(0, 1)
        load_keys(1)
        cap_all = keep.tile([P, H], BF16, name="cap_all")
        nc.sync.dma_start(out=cap_all[:], in_=cap.rearrange("h a b -> (h a b)").partition_broadcast(P))
        temp_sb = keep.tile([P, TILES], BF16, name="temp_sb")
        nc.sync.dma_start(out=temp_sb[:], in_=temp.rearrange("h (a m) o -> (h a) (m o)", m=TILES))
        load_queries(1, 2)
        load_queries(2, PAIRS)
        for g in range(2, GROUPS):
            load_keys(g)

        ident = keep.tile([P, P], F32, name="ident")
        make_identity(nc, ident[:])
        span = P // H
        head_mask = keep.tile([P, H], F32, name="head_mask")
        nc.gpsimd.memset(head_mask[:], 1.0)
        nc.gpsimd.affine_select(out=head_mask[:], in_=head_mask[:], pattern=[[-span, H]], compare_op=ALU.is_ge,
                                fill=0.0, base=0, channel_multiplier=1)
        nc.gpsimd.affine_select(out=head_mask[:], in_=head_mask[:], pattern=[[span, H]], compare_op=ALU.is_ge,
                                fill=0.0, base=span - 1, channel_multiplier=-1)
        mean_bank = psum.tile([P, 2, P], F32, name="mean_bank")
        for w in range(2):
            nc.tensor.transpose(mean_bank[:, w, :], mean_words[:, w:w + 1].to_broadcast([P, P]), ident[:])
        mean_row = mean_bank[:].rearrange("p w c -> p (w c)").bitcast(BF16)

        picked = keep.tile([P, H], F32, name="picked")
        cap_col = keep.tile([P, 1], F32, name="cap_col")
        inv_cap = keep.tile([P, 1], F32, name="inv_cap")
        slope = keep.tile([P, TILES], F32, name="slope")

        def copy_on(vector, out, in_):
            if vector:
                nc.vector.tensor_copy(out=out, in_=in_)
            else:
                nc.scalar.copy(out=out, in_=in_)

        def turn_rows(words):
            bank = psum.tile([P, 4, P], F32, name="turn", bufs=TURN_BANKS)
            for r in range(2):
                for u in range(2):
                    every_second = words[:, r * ROW_WORDS + u:(r + 1) * ROW_WORDS:2]
                    nc.tensor.transpose(bank[:, 2 * r + u, :], every_second, ident[:])
            return bank

        wide, value, key_bank, key_grouped, key_mx = {}, {}, {}, {}, {}

        def part_bytes(part):
            wide[part] = work.tile([P, 2 * D], BF16, name="wide", bufs=5)
            at = (part % 2) * 2 * D
            return key_bytes[part // 2][:, at:at + 2 * D].bitcast(FP8)

        def widen(part, vector=False):
            stored = part_bytes(part)
            copy_on(vector, wide[part][:], stored)

        def dequantise(part):
            value[part] = work.tile([P, 2 * D], BF16, name="value", bufs=4)
            for r in range(2):
                for b in range(BLOCKS):
                    cols = slice(r * D + b * B, r * D + (b + 1) * B)
                    at = BLOCKS * (2 * (part % 2) + r) + b
                    nc.vector.scalar_tensor_tensor(
                        out=value[part][:, cols], in0=wide[part][:, cols], scalar=key_scale[:, part // 2, at:at + 1],
                        in1=mean_row[:, b * B:(b + 1) * B], op0=ALU.mult, op1=ALU.add)

        def turn_keys(part):
            key_bank[part] = turn_rows(value[part][:].bitcast(F32))

        def copy_keys(part):
            g, half = divmod(part, 2)
            if half == 0:
                key_grouped[g] = work.tile([P, GROUP * PACK], BF16, name="key_grouped", align_bytes=64)
            words = key_grouped[g][:].bitcast(F32).rearrange("c (p w) -> c p w", w=2 * PACK)
            nc.scalar.copy(out=words[:, :, 4 * half:4 * half + 4], in_=key_bank[part][:].rearrange("c w p -> c p w"))

        def quantise_keys(g):
            codes = work.tile([P, GROUP], U32, name="key_codes", bufs=3, align_bytes=64)
            scales = work.tile([P, GROUP], U8, name="key_scales", bufs=3, align_bytes=64)
            nc.vector.quantize_mx(out=codes[:].bitcast(FP8X4), scales=scales[:], in_=key_grouped[g][:])
            key_mx[g] = (codes, scales)

        q_bank, q_grouped, q_mx = {}, {}, {}

        def turn_queries(pair):
            q_bank[pair] = turn_rows(q_words[pair])

        def copy_queries(pair, vector=False):
            q_grouped[pair] = keep.tile([P, 2 * P * PACK], BF16, name="q_grouped", bufs=PAIRS, align_bytes=64)
            copy_on(vector, q_grouped[pair][:].bitcast(F32).rearrange("c (r p u) -> c r p u", r=2, u=2),
                    q_bank[pair][:].rearrange("c (r u) p -> c r p u", u=2))

        def quantise_queries(pair):
            codes = keep.tile([P, 2 * P], U32, name="q_codes", bufs=PAIRS, align_bytes=64)
            scales = keep.tile([P, 2 * P], U8, name="q_scales", bufs=PAIRS, align_bytes=64)
            nc.vector.quantize_mx(out=codes[:].bitcast(FP8X4), scales=scales[:], in_=q_grouped[pair][:])
            q_mx[pair] = (codes, scales)

        raw, logits = {}, {}

        def multiply(n):
            g, m = divmod(n, TILES)
            raw[n] = psum.tile([P, GROUP], F32, name="raw", bufs=RAW_BANKS)
            cols = slice((m % 2) * P, (m % 2 + 1) * P)
            nc.tensor.matmul_mx(
                out=raw[n][:], lhsT=q_mx[m // 2][0][:, cols].bitcast(FP8X4), lhsT_scale=q_mx[m // 2][1][:, cols],
                rhs=key_mx[g][0][:].bitcast(FP8X4), rhs_scale=key_mx[g][1][:], start=True, stop=True)

        def squash(n):
            g, m = divmod(n, TILES)
            if m == 0:
                logits[g] = work.tile([P, TILES, GROUP], F32, name="logits", bufs=4)
            nc.scalar.activation(out=logits[g][:, m, :], in_=raw[n][:], func=ACT.Tanh, scale=slope[:, m:m + 1])

        def step_tiles(step, first, last):
            g, m = divmod(step * STEP_TILES, TILES)
            return g, slice(m + first, m + last)

        rounded = {}

        def round_y(step, first, last):
            g, tiles = step_tiles(step, first, last)
            if first == 0:
                rounded[step] = work.tile([P, 2, STEP_TILES, GROUP // 2], BF16, name="rounded", bufs=8)
            nc.vector.tensor_scalar(
                out=rounded[step][:, :, first:last, :].rearrange("q u m (p e) -> q u (m p) e", e=2),
                in0=logits[g][:, tiles, :].rearrange("q m (p u e) -> q u (m p) e", u=2, e=2),
                scalar1=cap_col[:], scalar2=None, op0=ALU.mult)

        def step_columns(step, first, last):
            g, tiles = step_tiles(step, 0, STEP_TILES)
            return logits[g][:, tiles, :].rearrange("q m s -> q (m s)")[:, first:last]

        def scale_on_gpsimd(step, cols):
            view = step_columns(step, 0, cols)
            nc.gpsimd.tensor_scalar(out=view, in0=view, scalar1=cap_col[:], scalar2=1.0, op0=ALU.mult, op1=ALU.mult)

        def scale_rest_and_store(step, done):
            view = step_columns(step, done, STEP_COLS)
            nc.vector.tensor_scalar(out=view, in0=view, scalar1=cap_col[:], scalar2=None, op0=ALU.mult)
            g, tiles = step_tiles(step, 0, STEP_TILES)
            nc.sync.dma_start(out=y_rows[:, tiles, g * GROUP:(g + 1) * GROUP], in_=logits[g][:, tiles, :])

        y_bank, y_grouped, y_scales = {}, {}, {}
        queue = {"turned": 0, "copied": 0, "quantised": 0}

        def turn_next(steps_rounded):
            n = queue["turned"]
            if n < 2 * steps_rounded and n - queue["copied"] < TURNED_AHEAD:
                y_bank[n] = psum.tile([P, 4, P], F32, name="turn", bufs=TURN_BANKS)
                for r in range(2):
                    for u in range(2):
                        words = rounded[n // 2][:, u, 2 * (n % 2) + r, :].bitcast(F32)
                        nc.tensor.transpose(y_bank[n][:, 2 * r + u, :], words, ident[:])
                queue["turned"] = n + 1

        def copy_next(vector):
            n = queue["copied"]
            if n < queue["turned"]:
                g, pair = divmod(n, PAIRS)
                if pair == 0:
                    y_grouped[g] = work.tile([P, H * T * PACK], BF16, name="y_grouped", bufs=3, align_bytes=64)
                words = y_grouped[g][:].bitcast(F32).rearrange("p (q w) -> p q w", w=2 * TILES)
                copy_on(vector, words[:, :, 4 * pair:4 * pair + 4], y_bank[n][:].rearrange("p w q -> p q w"))
                queue["copied"] = n + 1

        def quantise_next():
            g = queue["quantised"]
            if PAIRS * (g + 1) <= queue["copied"]:
                first, last = [batch for batch in SCALE_BATCHES if batch[0] <= g < batch[1]][0]
                if g == first:
                    y_scales[first] = keep.tile([P, last - first, H * T], U8, name="y_scales",
                                                bufs=len(SCALE_BATCHES), align_bytes=64)
                codes = work.tile([P, H * T], U32, name="y_codes", bufs=5, align_bytes=64)
                nc.vector.quantize_mx(out=codes[:].bitcast(FP8X4), scales=y_scales[first][:, g - first, :],
                                      in_=y_grouped[g][:])
                nc.sync.dma_start(out=out_1[g].rearrange("p m t -> p (m t)").bitcast(I32), in_=codes[:].bitcast(I32))
                if g == last - 1:
                    for quad in range(4):
                        rows = out_2[first:last, 4 * quad:4 * quad + 4, :].rearrange("g r m -> r g m")
                        nc.sync.dma_start(out=rows.bitcast(I32),
                                          in_=y_scales[first][32 * quad:32 * quad + 4, :, :].bitcast(I32))
                queue["quantised"] = g + 1

        widen(0, vector=True)
        stored = part_bytes(1)
        nc.scalar.activation(out=wide[1][:], in_=stored, func=ACT.Copy)
        dequantise(0)
        nc.vector.tensor_tensor(out=picked[:], in0=cap_all[:], in1=head_mask[:], op=ALU.mult)
        dequantise(1)
        nc.vector.tensor_reduce(out=cap_col[:], in_=picked[:], op=ALU.add, axis=mybir.AxisListType.X)
        turn_queries(0)
        turn_keys(0)
        turn_keys(1)
        turn_queries(1)
        widen(2)
        copy_queries(0)
        widen(3)
        copy_keys(0)
        copy_keys(1)
        quantise_queries(0)
        nc.vector.reciprocal(out=inv_cap[:], in_=cap_col[:])
        dequantise(2)
        nc.vector.tensor_scalar(out=slope[:], in0=temp_sb[:], scalar1=inv_cap[:], scalar2=None, op0=ALU.mult)
        quantise_keys(0)
        copy_queries(1)
        widen(4)
        turn_queries(2)
        multiply(0)
        multiply(1)
        quantise_queries(1)
        multiply(2)
        dequantise(3)
        copy_queries(2)
        squash(0)
        turn_queries(3)
        multiply(3)
        squash(1)
        dequantise(4)
        quantise_queries(2)
        turn_keys(2)
        multiply(4)
        copy_queries(3, vector=True)
        widen(5, vector=True)
        squash(2)
        turn_keys(3)
        multiply(5)
        quantise_queries(3)
        squash(3)
        copy_keys(2)
        multiply(6)
        turn_keys(4)
        copy_keys(3)

        for step in range(1, STEPS):
            part = step + PART_LEAD
            keys_left = part < PARTS
            odd = step % 2 == 1
            pool_cols = (POOL_COLS_LONG if odd else POOL_COLS_SHORT) if keys_left and step > 1 else 0
            split = -(-pool_cols // GROUP) if pool_cols else STEP_TILES // 2
            round_y(step - 1, 0, split)
            if pool_cols:
                scale_on_gpsimd(step - 1, pool_cols)
            round_y(step - 1, split, STEP_TILES)
            if step == 1:
                quantise_keys(1)
            if keys_left:
                dequantise(part)
            for i in range(STEP_TILES):
                n = step * STEP_TILES + i
                squash(n)
                if n + RAW_BANKS < GROUPS * TILES:
                    multiply(n + RAW_BANKS)
                if i == 0:
                    copy_next(vector=False)
                if i == 1:
                    if part - 1 < PARTS:
                        copy_keys(part - 1)
                    if keys_left and odd:
                        copy_next(vector=True)
                    scale_rest_and_store(step - 1, pool_cols)
                if i == 2 and part + 1 < PARTS:
                    widen(part + 1)
                if i == 2 and keys_left:
                    turn_keys(part)
                else:
                    turn_next(step)
                if i == 2:
                    if not odd and part - 1 < PARTS:
                        quantise_keys((part - 1) // 2)
                    if odd or not keys_left:
                        quantise_next()

        round_y(STEPS - 1, 0, STEP_TILES // 2)
        round_y(STEPS - 1, STEP_TILES // 2, STEP_TILES)
        scale_rest_and_store(STEPS - 1, 0)
        while queue["copied"] < PAIRS * GROUPS:
            copy_next(vector=False)
            turn_next(STEPS)
            turn_next(STEPS)
            quantise_next()
